import numpy as np
import ml_dtypes


def mxq(x, axis, fmt="e4m3"):
    dtype, down = {"e4m3": (ml_dtypes.float8_e4m3fn, 7), "e5m2": (ml_dtypes.float8_e5m2, 14)}[fmt]
    v = np.moveaxis(np.asarray(x, np.float32).astype(ml_dtypes.bfloat16).astype(np.float64), axis, -1)
    blocks = v.reshape(v.shape[:-1] + (-1, 32))
    amax = np.abs(blocks).max(-1, keepdims=True)
    byte = np.maximum(np.where(amax > 0, np.frexp(amax)[1] - 1 + 127, 0) - down, 1)
    scale = np.exp2(byte - 127.0)
    codes = (blocks / scale).astype(np.float32).astype(dtype).astype(np.float64)
    return np.moveaxis((codes * scale).reshape(v.shape), -1, axis)


WIDE = False


def mx_kscale(k):
    if not WIDE:
        return np.ones(k)
    levels = np.array([10, -10, 5, -5, 0])
    if k % 512:
        return np.exp2(np.random.permutation(np.resize(levels, k // 32))).repeat(32)
    a = np.empty((k // 512, 16))
    for p in range(k // 512):
        a[p, :8] = np.random.permutation(np.resize(levels, 8))
        for g in range(8):
            far = levels[np.abs(levels - a[p, g]) >= 10]
            a[p, g + 8] = far[np.random.randint(len(far))]
    return np.exp2(a.ravel()).repeat(32)


def f64(x):
    return np.asarray(x).astype(np.float64)


def striped(idx):
    return np.tile(idx.reshape(-1, 16).T, (8, 1)).astype(np.uint16)


def unstriped(offs):
    return offs[:16].T.reshape(-1).astype(np.int64)


def relu(v):
    return np.maximum(v, 0.0)


K, T, S, H, N = 512, 2048, 768, 1024, 512


def setup_inputs():
    n = np.random.standard_normal
    s = mx_kscale(K)[:, None]
    u = mx_kscale(H)
    return {
        "xT": (n((K, T)) * s).astype(np.float32),
        "w1": (n((K, H)) / np.sqrt(K) / s * u).astype(np.float32),
        "w2": (n((H, N)) / np.sqrt(H) / u[:, None]).astype(np.float32),
        "offs": striped(np.sort(np.random.permutation(T)[:S])),
    }


def reference(xT, w1, w2, offs):
    idx = unstriped(offs)
    xq = mxq(f64(xT)[:, idx], 0, "e4m3")
    h = relu(mxq(f64(w1), 0, "e4m3").T @ xq)
    y = mxq(f64(w2), 0, "e4m3").T @ mxq(h, 0, "e4m3")
    return y

@@ -1,0 +1,216 @@
+from contextlib import ExitStack
+
+import concourse.mybir as mybir
+
+K, T, S, H, N = 512, 2048, 768, 1024, 512
+FLOPS = 2 * S * K * H + 2 * S * H * N
+
+P = 128
+PACK = 4
+HALF = P * PACK
+HALVES = H // HALF
+PIECE = 256
+PIECES = S // PIECE
+BLOCK = 128
+WIDE = 2 * PIECE
+
+F32 = mybir.dt.float32
+BF16 = mybir.dt.bfloat16
+U32 = mybir.dt.uint32
+U16 = mybir.dt.uint16
+U8 = mybir.dt.uint8
+FP8X4 = mybir.dt.float8_e4m3fn_x4
+RELU = mybir.ActivationFunctionType.Relu
+
+
+def tile_picked_pick_mlp_relu_srt_e_kernel(tc, xT, w1, w2, offs, out):
+    nc = tc.nc
+    with ExitStack() as ctx:
+        held = ctx.enter_context(tc.tile_pool(name="held", bufs=1))
+        psum = ctx.enter_context(tc.psum_pool(name="psum", bufs=8))
+
+        def words(width, name):
+            return held.tile([P, width], U32, name=name, align_bytes=64)
+
+        def scale_bytes(width, name):
+            return held.tile([P, width], U8, name=name, align_bytes=64)
+
+        def bf16_values(width, name):
+            return held.tile([P, PACK * width], BF16, name=name, align_bytes=64)
+
+        offsets = held.tile([P, S // 16], U16, name="offsets")
+        planes = [held.tile([P, T], F32, name=f"plane{j}", align_bytes=64) for j in range(PACK)]
+        picked = held.tile([P, PACK, S], F32, name="picked", align_bytes=64)
+        raw_w1 = [held.tile([P, PACK, HALF], F32, name=f"raw_w1_{g}") for g in range(HALVES)]
+        raw_w2 = [held.tile([P, PACK, N], F32, name=f"raw_w2_{g}") for g in range(HALVES)]
+        x_bf = [bf16_values(PIECE, f"x_bf{s}") for s in range(PIECES)]
+        x_codes = [words(PIECE, f"x_codes{s}") for s in range(PIECES)]
+        x_scales = [scale_bytes(PIECE, f"x_scales{s}") for s in range(PIECES)]
+        w1_bf = [bf16_values(HALF, f"w1_bf{g}") for g in range(HALVES)]
+        w1_codes = [words(HALF, f"w1_codes{g}") for g in range(HALVES)]
+        w1_scales = [scale_bytes(HALF, f"w1_scales{g}") for g in range(HALVES)]
+        w2_bf = [bf16_values(N, f"w2_bf{g}") for g in range(HALVES)]
+        w2_codes = [words(N, f"w2_codes{g}") for g in range(HALVES)]
+        w2_scales = [scale_bytes(N, f"w2_scales{g}") for g in range(HALVES)]
+        h_bf = [[bf16_values(PIECE, f"h_bf{g}{s}") for s in range(PIECES)] for g in range(HALVES)]
+        h_codes = [words(S, f"h_codes{g}") for g in range(HALVES)]
+        h_scales = [scale_bytes(S, f"h_scales{g}") for g in range(HALVES)]
+
+        x_rows = xT.rearrange("(p j) w -> p j w", j=PACK)
+        w1_rows = w1.rearrange("(p j) i -> p j i", j=PACK)
+        w2_rows = w2.rearrange("(g p j) m -> g p j m", g=HALVES, j=PACK)
+        first_part = T - S + PIECE
+        nc.sync.dma_start(planes[0][:], x_rows[:, 0, :])
+        nc.sync.dma_start(offsets[:], offs)
+        nc.sync.dma_start(planes[1][:], x_rows[:, 1, :])
+        nc.sync.dma_start(planes[2][:], x_rows[:, 2, :])
+        nc.sync.dma_start(planes[3][:, :first_part], x_rows[:, 3, :first_part])
+        nc.sync.dma_start(planes[3][:, first_part:], x_rows[:, 3, first_part:])
+        for g in range(HALVES):
+            nc.sync.dma_start(raw_w1[g][:], w1_rows[:, :, HALF * g : HALF * (g + 1)])
+        for g in range(HALVES):
+            nc.sync.dma_start(raw_w2[g][:], w2_rows[g])
+
+        warm_in = held.tile([P, 1], F32, name="warm_in")
+        warm_out = held.tile([P, 1], F32, name="warm_out")
+        nc.vector.memset(warm_in[:], 0.0)
+        nc.scalar.activation(warm_out[:], warm_in[:], RELU)
+
+        def copy(engine, dst, src):
+            if engine == "scalar":
+                nc.scalar.copy(dst, src)
+            else:
+                nc.vector.tensor_copy(dst, src)
+
+        def quantise(codes, scales, values):
+            nc.vector.quantize_mx(out=codes.bitcast(FP8X4), scales=scales, in_=values)
+
+        def gather_plane(j):
+            nc.vector.tensor_copy(picked[:, j, :], planes[j][:].indirect(offsets[:]))
+
+        def gather_last_plane(s):
+            entries = slice(PIECE * s, PIECE * (s + 1))
+            window = T - S + PIECE * (s + 1)
+            nc.vector.tensor_copy(
+                picked[:, PACK - 1, entries],
+                planes[PACK - 1][:, :window].indirect(offsets[:, PIECE * s // 16 : PIECE * (s + 1) // 16]),
+            )
+
+        def interleave(engine, dst, src):
+            copy(
+                engine,
+                dst.rearrange("p (q c j) -> p q j c", c=4, j=PACK),
+                src.rearrange("p j (q c) -> p q j c", c=4),
+            )
+
+        def interleave_x(engine, s, lo, hi):
+            interleave(engine, x_bf[s][:, PACK * lo : PACK * hi], picked[:, :, PIECE * s + lo : PIECE * s + hi])
+
+        def quantise_x(s):
+            quantise(x_codes[s][:], x_scales[s][:], x_bf[s][:])
+
+        def interleave_w1(engine, g, lo, hi):
+            dst = w1_bf[g][:].rearrange("p (t m j) -> p m j t", t=PACK, j=PACK)
+            src = raw_w1[g][:].rearrange("p j (m t) -> p m j t", t=PACK)
+            copy(engine, dst[:, lo:hi], src[:, lo:hi])
+
+        def quantise_w1(g, lo, hi):
+            quantise(w1_codes[g][:, lo:hi], w1_scales[g][:, lo:hi], w1_bf[g][:, PACK * lo : PACK * hi])
+
+        def interleave_w2(engine, g, lo, hi):
+            interleave(engine, w2_bf[g][:, PACK * lo : PACK * hi], raw_w2[g][:, :, lo:hi])
+
+        def quantise_w2(g, lo, hi):
+            quantise(w2_codes[g][:, lo:hi], w2_scales[g][:, lo:hi], w2_bf[g][:, PACK * lo : PACK * hi])
+
+        def layer1(g, s, b):
+            bank = psum.tile([P, PACK, BLOCK], F32, name="bank")
+            tokens = slice(BLOCK * b, BLOCK * (b + 1))
+            for t in range(PACK):
+                channels = slice(P * t, P * (t + 1))
+                nc.tensor.matmul_mx(
+                    out=bank[:, t, :],
+                    lhsT=w1_codes[g][:, channels].bitcast(FP8X4),
+                    lhsT_scale=w1_scales[g][:, channels],
+                    rhs=x_codes[s][:, tokens].bitcast(FP8X4),
+                    rhs_scale=x_scales[s][:, tokens],
+                    start=True,
+                    stop=True,
+                )
+            dst = h_bf[g][s][:, PACK * BLOCK * b : PACK * BLOCK * (b + 1)]
+            nc.scalar.activation(
+                dst.rearrange("p (n t) -> p n t", t=PACK), bank[:].rearrange("p t n -> p n t"), RELU
+            )
+
+        def quantise_h(g, s):
+            entries = slice(PIECE * s, PIECE * (s + 1))
+            quantise(h_codes[g][:, entries], h_scales[g][:, entries], h_bf[g][s][:])
+
+        def layer2(engine, m, lo, hi):
+            bank = psum.tile([P, hi - lo], F32, name="bank")
+            rows = slice(P * m, P * (m + 1))
+            for g in range(HALVES):
+                nc.tensor.matmul_mx(
+                    out=bank[:],
+                    lhsT=w2_codes[g][:, rows].bitcast(FP8X4),
+                    lhsT_scale=w2_scales[g][:, rows],
+                    rhs=h_codes[g][:, lo:hi].bitcast(FP8X4),
+                    rhs_scale=h_scales[g][:, lo:hi],
+                    start=(g == 0),
+                    stop=(g == HALVES - 1),
+                )
+            result = held.tile([P, hi - lo], F32, name=f"result{m}_{lo}")
+            copy(engine, result[:], bank[:])
+            nc.sync.dma_start(out[rows, lo:hi], result[:])
+
+        gather_plane(0)
+        gather_plane(1)
+        gather_plane(2)
+        gather_last_plane(0)
+        gather_last_plane(1)
+        interleave_x("vector", 1, 0, 192)
+        interleave_x("scalar", 0, 0, 256)
+        interleave_x("scalar", 1, 192, 256)
+        gather_last_plane(2)
+        interleave_w1("scalar", 0, 112, 128)
+        interleave_w1("vector", 0, 0, 112)
+        quantise_w1(0, 0, 256)
+        quantise_w1(0, 256, 512)
+        quantise_x(0)
+        interleave_x("scalar", 2, 0, 256)
+        quantise_x(1)
+        layer1(0, 0, 0)
+        layer1(0, 1, 0)
+        interleave_w1("vector", 1, 0, 128)
+        quantise_w1(1, 0, 512)
+        layer1(1, 0, 0)
+        layer1(1, 0, 1)
+        layer1(0, 0, 1)
+        quantise_x(2)
+        layer1(1, 1, 0)
+        interleave_w2("vector", 0, 0, 512)
+        layer1(1, 1, 1)
+        layer1(0, 1, 1)
+        quantise_h(0, 1)
+        quantise_h(0, 0)
+        interleave_w2("scalar", 1, 320, 512)
+        layer1(0, 2, 0)
+        layer1(1, 2, 0)
+        quantise_w2(0, 0, 512)
+        layer1(0, 2, 1)
+        interleave_w2("vector", 1, 0, 320)
+        quantise_h(1, 1)
+        quantise_w2(1, 0, 256)
+        quantise_w2(1, 256, 512)
+        layer1(1, 2, 1)
+        quantise_h(1, 0)
+        layer2("vector", 0, 0, WIDE)
+        layer2("vector", 1, 0, WIDE)
+        quantise_h(0, 2)
+        layer2("scalar", 2, 0, WIDE)
+        layer2("scalar", 3, 0, WIDE)
+        quantise_h(1, 2)
+        layer2("vector", 0, WIDE, S)
+        layer2("scalar", 1, WIDE, S)
+        layer2("vector", 2, WIDE, S)
+        layer2("scalar", 3, WIDE, S)

@@ -12,7 +12,9 @@ HALVES = H // HALF
 PIECE = 256
 PIECES = S // PIECE
 BLOCK = 128
+PART = 256
 WIDE = 2 * PIECE
+RUN = 4
 
 F32 = mybir.dt.float32
 BF16 = mybir.dt.bfloat16
@@ -21,6 +23,7 @@ U16 = mybir.dt.uint16
 U8 = mybir.dt.uint8
 FP8X4 = mybir.dt.float8_e4m3fn_x4
 RELU = mybir.ActivationFunctionType.Relu
+MAX = mybir.AluOpType.max
 
 
 def tile_picked_pick_mlp_relu_srt_e_kernel(tc, xT, w1, w2, offs, out):
@@ -41,35 +44,53 @@ def tile_picked_pick_mlp_relu_srt_e_kernel(tc, xT, w1, w2, offs, out):
         offsets = held.tile([P, S // 16], U16, name="offsets")
         planes = [held.tile([P, T], F32, name=f"plane{j}", align_bytes=64) for j in range(PACK)]
         picked = held.tile([P, PACK, S], F32, name="picked", align_bytes=64)
-        raw_w1 = [held.tile([P, PACK, HALF], F32, name=f"raw_w1_{g}") for g in range(HALVES)]
-        raw_w2 = [held.tile([P, PACK, N], F32, name=f"raw_w2_{g}") for g in range(HALVES)]
-        x_bf = [bf16_values(PIECE, f"x_bf{s}") for s in range(PIECES)]
-        x_codes = [words(PIECE, f"x_codes{s}") for s in range(PIECES)]
-        x_scales = [scale_bytes(PIECE, f"x_scales{s}") for s in range(PIECES)]
+        x_bf = bf16_values(S, "x_bf")
+        x_codes = {}
+        x_scales = scale_bytes(S, "x_scales")
         w1_bf = [bf16_values(HALF, f"w1_bf{g}") for g in range(HALVES)]
         w1_codes = [words(HALF, f"w1_codes{g}") for g in range(HALVES)]
         w1_scales = [scale_bytes(HALF, f"w1_scales{g}") for g in range(HALVES)]
         w2_bf = [bf16_values(N, f"w2_bf{g}") for g in range(HALVES)]
         w2_codes = [words(N, f"w2_codes{g}") for g in range(HALVES)]
         w2_scales = [scale_bytes(N, f"w2_scales{g}") for g in range(HALVES)]
-        h_bf = [[bf16_values(PIECE, f"h_bf{g}{s}") for s in range(PIECES)] for g in range(HALVES)]
-        h_codes = [words(S, f"h_codes{g}") for g in range(HALVES)]
+        h_bf = [bf16_values(S, f"h_bf{g}") for g in range(HALVES)]
         h_scales = [scale_bytes(S, f"h_scales{g}") for g in range(HALVES)]
+        raw = {}
 
         x_rows = xT.rearrange("(p j) w -> p j w", j=PACK)
         w1_rows = w1.rearrange("(p j) i -> p j i", j=PACK)
         w2_rows = w2.rearrange("(g p j) m -> g p j m", g=HALVES, j=PACK)
-        first_part = T - S + PIECE
-        nc.sync.dma_start(planes[0][:], x_rows[:, 0, :])
+
+        def load_plane(j, lo, hi):
+            nc.sync.dma_start(planes[j][:, lo:hi], x_rows[:, j, lo:hi])
+
+        def load_w1(g, lo, hi):
+            raw["w1", g, lo] = held.tile([P, PACK, hi - lo], F32, name=f"raw_w1_{g}_{lo}", align_bytes=64)
+            nc.sync.dma_start(raw["w1", g, lo][:], w1_rows[:, :, HALF * g + lo : HALF * g + hi])
+
+        def load_w2(g, lo, hi):
+            raw["w2", g, lo] = held.tile([P, PACK, hi - lo], F32, name=f"raw_w2_{g}_{lo}")
+            nc.sync.dma_start(raw["w2", g, lo][:], w2_rows[g][:, :, lo:hi])
+
+        load_plane(0, 0, T)
         nc.sync.dma_start(offsets[:], offs)
-        nc.sync.dma_start(planes[1][:], x_rows[:, 1, :])
-        nc.sync.dma_start(planes[2][:], x_rows[:, 2, :])
-        nc.sync.dma_start(planes[3][:, :first_part], x_rows[:, 3, :first_part])
-        nc.sync.dma_start(planes[3][:, first_part:], x_rows[:, 3, first_part:])
-        for g in range(HALVES):
-            nc.sync.dma_start(raw_w1[g][:], w1_rows[:, :, HALF * g : HALF * (g + 1)])
-        for g in range(HALVES):
-            nc.sync.dma_start(raw_w2[g][:], w2_rows[g])
+        load_plane(1, 0, T)
+        load_plane(2, 0, T)
+        load_plane(3, 0, T - S + PIECE)
+        load_plane(3, T - S + PIECE, T)
+        load_w1(0, 0, PART)
+        load_w1(0, PART, HALF)
+        load_w1(1, 0, PART)
+        load_w1(1, PART, HALF)
+        load_w2(0, 0, PART)
+        load_w2(1, 0, PART)
+        load_w2(0, PART, N)
+        load_w2(1, PART, N)
+
+        h_codes = [
+            held.tile([P, S], U32, name="h_codes0", tag=f"raw_w1_1_{PART}", align_bytes=64),
+            words(S, "h_codes1"),
+        ]
 
         warm_in = held.tile([P, 1], F32, name="warm_in")
         warm_out = held.tile([P, 1], F32, name="warm_out")
@@ -82,135 +103,155 @@ def tile_picked_pick_mlp_relu_srt_e_kernel(tc, xT, w1, w2, offs, out):
             else:
                 nc.vector.tensor_copy(dst, src)
 
-        def quantise(codes, scales, values):
-            nc.vector.quantize_mx(out=codes.bitcast(FP8X4), scales=scales, in_=values)
+        def quantise(codes, scales, values, lo, hi):
+            nc.vector.quantize_mx(
+                out=codes[:, lo:hi].bitcast(FP8X4), scales=scales[:, lo:hi], in_=values[:, PACK * lo : PACK * hi]
+            )
 
-        def gather_plane(j):
-            nc.vector.tensor_copy(picked[:, j, :], planes[j][:].indirect(offsets[:]))
-
-        def gather_last_plane(s):
-            entries = slice(PIECE * s, PIECE * (s + 1))
-            window = T - S + PIECE * (s + 1)
+        def gather(j, lo, hi):
             nc.vector.tensor_copy(
-                picked[:, PACK - 1, entries],
-                planes[PACK - 1][:, :window].indirect(offsets[:, PIECE * s // 16 : PIECE * (s + 1) // 16]),
+                picked[:, j, lo:hi], planes[j][:, : T - S + hi].indirect(offsets[:, lo // 16 : hi // 16])
             )
 
         def interleave(engine, dst, src):
             copy(
                 engine,
-                dst.rearrange("p (q c j) -> p q j c", c=4, j=PACK),
-                src.rearrange("p j (q c) -> p q j c", c=4),
+                dst.rearrange("p (q c j) -> p q j c", c=RUN, j=PACK),
+                src.rearrange("p j (q c) -> p q j c", c=RUN),
             )
 
-        def interleave_x(engine, s, lo, hi):
-            interleave(engine, x_bf[s][:, PACK * lo : PACK * hi], picked[:, :, PIECE * s + lo : PIECE * s + hi])
+        def cast_x(engine, lo, hi):
+            interleave(engine, x_bf[:, PACK * lo : PACK * hi], picked[:, :, lo:hi])
 
-        def quantise_x(s):
-            quantise(x_codes[s][:], x_scales[s][:], x_bf[s][:])
+        def quantise_x(lo, hi):
+            x_codes[lo] = held.tile([P, hi - lo], U32, name=f"x_codes{lo}", tag=f"raw_w1_0_{lo}", align_bytes=64)
+            nc.vector.quantize_mx(
+                out=x_codes[lo][:].bitcast(FP8X4), scales=x_scales[:, lo:hi], in_=x_bf[:, PACK * lo : PACK * hi]
+            )
 
-        def interleave_w1(engine, g, lo, hi):
+        def cast_w1(engine, g, base, lo, hi):
             dst = w1_bf[g][:].rearrange("p (t m j) -> p m j t", t=PACK, j=PACK)
-            src = raw_w1[g][:].rearrange("p j (m t) -> p m j t", t=PACK)
-            copy(engine, dst[:, lo:hi], src[:, lo:hi])
+            src = raw["w1", g, base][:].rearrange("p j (m t) -> p m j t", t=PACK)
+            copy(engine, dst[:, lo // PACK : hi // PACK], src[:, (lo - base) // PACK : (hi - base) // PACK])
 
         def quantise_w1(g, lo, hi):
-            quantise(w1_codes[g][:, lo:hi], w1_scales[g][:, lo:hi], w1_bf[g][:, PACK * lo : PACK * hi])
+            quantise(w1_codes[g], w1_scales[g], w1_bf[g], lo, hi)
 
-        def interleave_w2(engine, g, lo, hi):
-            interleave(engine, w2_bf[g][:, PACK * lo : PACK * hi], raw_w2[g][:, :, lo:hi])
+        def cast_w2(engine, g, base, lo, hi):
+            interleave(engine, w2_bf[g][:, PACK * lo : PACK * hi], raw["w2", g, base][:, :, lo - base : hi - base])
 
         def quantise_w2(g, lo, hi):
-            quantise(w2_codes[g][:, lo:hi], w2_scales[g][:, lo:hi], w2_bf[g][:, PACK * lo : PACK * hi])
+            quantise(w2_codes[g], w2_scales[g], w2_bf[g], lo, hi)
 
-        def layer1(g, s, b):
+        def layer1_block(engine, g, lo):
             bank = psum.tile([P, PACK, BLOCK], F32, name="bank")
-            tokens = slice(BLOCK * b, BLOCK * (b + 1))
+            tokens = slice(lo, lo + BLOCK)
+            base = min(lo // PIECE, 1) * PIECE
             for t in range(PACK):
                 channels = slice(P * t, P * (t + 1))
                 nc.tensor.matmul_mx(
                     out=bank[:, t, :],
                     lhsT=w1_codes[g][:, channels].bitcast(FP8X4),
                     lhsT_scale=w1_scales[g][:, channels],
-                    rhs=x_codes[s][:, tokens].bitcast(FP8X4),
-                    rhs_scale=x_scales[s][:, tokens],
+                    rhs=x_codes[base][:, lo - base : lo - base + BLOCK].bitcast(FP8X4),
+                    rhs_scale=x_scales[:, tokens],
                     start=True,
                     stop=True,
                 )
-            dst = h_bf[g][s][:, PACK * BLOCK * b : PACK * BLOCK * (b + 1)]
-            nc.scalar.activation(
-                dst.rearrange("p (n t) -> p n t", t=PACK), bank[:].rearrange("p t n -> p n t"), RELU
+            dst = h_bf[g][:, PACK * lo : PACK * (lo + BLOCK)].rearrange("p (n t) -> p n t", t=PACK)
+            src = bank[:].rearrange("p t n -> p n t")
+            if engine == "scalar":
+                nc.scalar.activation(dst, src, RELU)
+            else:
+                nc.vector.tensor_scalar_max(dst, src, 0.0)
+
+        def layer1(engine, g, s):
+            for lo in range(PIECE * s, PIECE * (s + 1), BLOCK):
+                layer1_block(engine, g, lo)
+
+        def quantise_h(g, lo, hi):
+            quantise(h_codes[g], h_scales[g], h_bf[g], lo, hi)
+
+        def layer2_pass(dst, g, m, lo, hi):
+            rows = slice(P * m, P * (m + 1))
+            nc.tensor.matmul_mx(
+                out=dst,
+                lhsT=w2_codes[g][:, rows].bitcast(FP8X4),
+                lhsT_scale=w2_scales[g][:, rows],
+                rhs=h_codes[g][:, lo:hi].bitcast(FP8X4),
+                rhs_scale=h_scales[g][:, lo:hi],
+                start=(g == 0),
+                stop=(g == HALVES - 1),
             )
 
-        def quantise_h(g, s):
-            entries = slice(PIECE * s, PIECE * (s + 1))
-            quantise(h_codes[g][:, entries], h_scales[g][:, entries], h_bf[g][s][:])
+        open_banks = {}
 
-        def layer2(engine, m, lo, hi):
-            bank = psum.tile([P, hi - lo], F32, name="bank")
-            rows = slice(P * m, P * (m + 1))
-            for g in range(HALVES):
-                nc.tensor.matmul_mx(
-                    out=bank[:],
-                    lhsT=w2_codes[g][:, rows].bitcast(FP8X4),
-                    lhsT_scale=w2_scales[g][:, rows],
-                    rhs=h_codes[g][:, lo:hi].bitcast(FP8X4),
-                    rhs_scale=h_scales[g][:, lo:hi],
-                    start=(g == 0),
-                    stop=(g == HALVES - 1),
-                )
+        def first_pass(m, lo, hi):
+            open_banks[m, lo] = psum.tile([P, hi - lo], F32, name="bank")
+            layer2_pass(open_banks[m, lo][:], 0, m, lo, hi)
+
+        def last_pass(engine, m, lo, hi):
+            bank = open_banks[m, lo]
+            layer2_pass(bank[:], 1, m, lo, hi)
             result = held.tile([P, hi - lo], F32, name=f"result{m}_{lo}")
             copy(engine, result[:], bank[:])
-            nc.sync.dma_start(out[rows, lo:hi], result[:])
+            nc.sync.dma_start(out[P * m : P * (m + 1), lo:hi], result[:])
 
-        gather_plane(0)
-        gather_plane(1)
-        gather_plane(2)
-        gather_last_plane(0)
-        gather_last_plane(1)
-        interleave_x("vector", 1, 0, 192)
-        interleave_x("scalar", 0, 0, 256)
-        interleave_x("scalar", 1, 192, 256)
-        gather_last_plane(2)
-        interleave_w1("scalar", 0, 112, 128)
-        interleave_w1("vector", 0, 0, 112)
-        quantise_w1(0, 0, 256)
-        quantise_w1(0, 256, 512)
-        quantise_x(0)
-        interleave_x("scalar", 2, 0, 256)
-        quantise_x(1)
-        layer1(0, 0, 0)
-        layer1(0, 1, 0)
-        interleave_w1("vector", 1, 0, 128)
-        quantise_w1(1, 0, 512)
-        layer1(1, 0, 0)
-        layer1(1, 0, 1)
-        layer1(0, 0, 1)
-        quantise_x(2)
-        layer1(1, 1, 0)
-        interleave_w2("vector", 0, 0, 512)
-        layer1(1, 1, 1)
-        layer1(0, 1, 1)
-        quantise_h(0, 1)
-        quantise_h(0, 0)
-        interleave_w2("scalar", 1, 320, 512)
-        layer1(0, 2, 0)
-        layer1(1, 2, 0)
-        quantise_w2(0, 0, 512)
-        layer1(0, 2, 1)
-        interleave_w2("vector", 1, 0, 320)
-        quantise_h(1, 1)
-        quantise_w2(1, 0, 256)
-        quantise_w2(1, 256, 512)
-        layer1(1, 2, 1)
-        quantise_h(1, 0)
-        layer2("vector", 0, 0, WIDE)
-        layer2("vector", 1, 0, WIDE)
-        quantise_h(0, 2)
-        layer2("scalar", 2, 0, WIDE)
-        layer2("scalar", 3, 0, WIDE)
-        quantise_h(1, 2)
-        layer2("vector", 0, WIDE, S)
-        layer2("scalar", 1, WIDE, S)
-        layer2("vector", 2, WIDE, S)
-        layer2("scalar", 3, WIDE, S)
+        def layer2_pair(engine, m0, lo, hi):
+            bank = psum.tile([P, 2, hi - lo], F32, name="bank")
+            for d in range(2):
+                for g in range(HALVES):
+                    layer2_pass(bank[:, d, :], g, m0 + d, lo, hi)
+            result = held.tile([P, 2, hi - lo], F32, name=f"pair{m0}_{lo}")
+            copy(engine, result[:], bank[:])
+            rows = out[P * m0 : P * (m0 + 2), lo:hi].rearrange("(d p) n -> p d n", d=2)
+            nc.sync.dma_start(rows, result[:])
+
+        for j in range(PACK - 1):
+            gather(j, 0, S)
+        for s in range(PIECES):
+            gather(PACK - 1, PIECE * s, PIECE * (s + 1))
+        cast_x("scalar", 0, PIECE)
+        cast_w1("vector", 0, 0, 0, PART)
+        quantise_x(0, PIECE)
+        cast_x("scalar", PIECE, WIDE)
+        cast_w1("vector", 0, PART, PART, HALF)
+        quantise_w1(0, 0, PART)
+        quantise_w1(0, PART, HALF)
+        cast_x("scalar", WIDE, S)
+        quantise_x(PIECE, S)
+        cast_w1("scalar", 1, 0, 0, 192)
+        layer1("scalar", 0, 0)
+        cast_w1("vector", 1, 0, 192, PART)
+        layer1("scalar", 0, 1)
+        cast_w1("vector", 1, PART, PART, HALF)
+        quantise_w1(1, 0, PART)
+        quantise_w1(1, PART, HALF)
+        layer1("scalar", 1, 0)
+        layer1("scalar", 1, 1)
+        cast_w2("vector", 0, 0, 0, PART)
+        quantise_h(0, 0, PIECE)
+        cast_w2("vector", 1, 0, 0, PART)
+        quantise_w2(0, 0, PART)
+        quantise_h(1, 0, PIECE)
+        quantise_w2(1, 0, PART)
+        quantise_h(0, PIECE, WIDE)
+        layer2_pair("scalar", 0, 0, PIECE)
+        layer1("scalar", 0, 2)
+        layer1("scalar", 1, 2)
+        cast_w2("vector", 0, PART, PART, N)
+        quantise_h(1, PIECE, WIDE)
+        quantise_w2(0, PART, N)
+        for m in (2, 3):
+            first_pass(m, 0, WIDE)
+        cast_w2("vector", 1, PART, PART, N)
+        quantise_h(0, WIDE, S)
+        quantise_w2(1, PART, N)
+        layer2_pair("vector", 0, PIECE, WIDE)
+        last_pass("scalar", 2, 0, WIDE)
+        quantise_h(1, WIDE, S)
+        last_pass("scalar", 3, 0, WIDE)
+        for m in range(4):
+            first_pass(m, WIDE, S)
+        for m in range(4):
+            last_pass("scalar" if m % 2 else "vector", m, WIDE, S)

@@ -14,6 +14,10 @@ PIECES = S // PIECE
 BLOCK = 128
 PART = 256
 WIDE = 2 * PIECE
+PAIR = 2
+BANK_BYTES = 2048
+LAYER1_BANKS = 4
+SHARE = 64
 RUN = 4
 
 F32 = mybir.dt.float32
@@ -23,39 +27,45 @@ U16 = mybir.dt.uint16
 U8 = mybir.dt.uint8
 FP8X4 = mybir.dt.float8_e4m3fn_x4
 RELU = mybir.ActivationFunctionType.Relu
-MAX = mybir.AluOpType.max
 
 
 def tile_picked_pick_mlp_relu_srt_e_kernel(tc, xT, w1, w2, offs, out):
     nc = tc.nc
     with ExitStack() as ctx:
         held = ctx.enter_context(tc.tile_pool(name="held", bufs=1))
-        psum = ctx.enter_context(tc.psum_pool(name="psum", bufs=8))
+        shared = ctx.enter_context(tc.tile_pool(name="shared", bufs=1))
+        psum = ctx.enter_context(tc.psum_pool(name="psum", bufs=1))
 
-        def words(width, name):
-            return held.tile([P, width], U32, name=name, align_bytes=64)
+        def words(width, name, tag=None):
+            return held.tile([P, width], U32, name=name, tag=tag or name, align_bytes=64)
 
         def scale_bytes(width, name):
             return held.tile([P, width], U8, name=name, align_bytes=64)
 
-        def bf16_values(width, name):
-            return held.tile([P, PACK * width], BF16, name=name, align_bytes=64)
+        def bf16_values(width, name, tag=None):
+            return held.tile([P, PACK * width], BF16, name=name, tag=tag or name, align_bytes=64)
+
+        def raw_rows(width, name):
+            return held.tile([P, PACK, width], F32, name=name, align_bytes=64)
 
         offsets = held.tile([P, S // 16], U16, name="offsets")
         planes = [held.tile([P, T], F32, name=f"plane{j}", align_bytes=64) for j in range(PACK)]
-        picked = held.tile([P, PACK, S], F32, name="picked", align_bytes=64)
-        x_bf = bf16_values(S, "x_bf")
+        picked = raw_rows(S, "picked")
+        x_bf = [bf16_values(PIECE, f"x_bf{s}") for s in range(PIECES)]
         x_codes = {}
         x_scales = scale_bytes(S, "x_scales")
-        w1_bf = [bf16_values(HALF, f"w1_bf{g}") for g in range(HALVES)]
+        w1_raw = [raw_rows(HALF, f"w1_raw{g}") for g in range(HALVES)]
+        w1_bf = {}
         w1_codes = [words(HALF, f"w1_codes{g}") for g in range(HALVES)]
         w1_scales = [scale_bytes(HALF, f"w1_scales{g}") for g in range(HALVES)]
-        w2_bf = [bf16_values(N, f"w2_bf{g}") for g in range(HALVES)]
+        w2_first = raw_rows(N, "w2_first")
+        w2_second = [raw_rows(PART, f"w2_second{a}") for a in range(N // PART)]
+        w2_bf = {}
         w2_codes = [words(N, f"w2_codes{g}") for g in range(HALVES)]
         w2_scales = [scale_bytes(N, f"w2_scales{g}") for g in range(HALVES)]
-        h_bf = [bf16_values(S, f"h_bf{g}") for g in range(HALVES)]
+        h_bf = [[bf16_values(PIECE, f"h_bf{g}{s}") for s in range(PIECES)] for g in range(HALVES)]
+        h_codes = {}
         h_scales = [scale_bytes(S, f"h_scales{g}") for g in range(HALVES)]
-        raw = {}
 
         x_rows = xT.rearrange("(p j) w -> p j w", j=PACK)
         w1_rows = w1.rearrange("(p j) i -> p j i", j=PACK)
@@ -64,33 +74,17 @@ def tile_picked_pick_mlp_relu_srt_e_kernel(tc, xT, w1, w2, offs, out):
         def load_plane(j, lo, hi):
             nc.sync.dma_start(planes[j][:, lo:hi], x_rows[:, j, lo:hi])
 
-        def load_w1(g, lo, hi):
-            raw["w1", g, lo] = held.tile([P, PACK, hi - lo], F32, name=f"raw_w1_{g}_{lo}", align_bytes=64)
-            nc.sync.dma_start(raw["w1", g, lo][:], w1_rows[:, :, HALF * g + lo : HALF * g + hi])
-
-        def load_w2(g, lo, hi):
-            raw["w2", g, lo] = held.tile([P, PACK, hi - lo], F32, name=f"raw_w2_{g}_{lo}")
-            nc.sync.dma_start(raw["w2", g, lo][:], w2_rows[g][:, :, lo:hi])
-
         load_plane(0, 0, T)
         nc.sync.dma_start(offsets[:], offs)
         load_plane(1, 0, T)
         load_plane(2, 0, T)
         load_plane(3, 0, T - S + PIECE)
         load_plane(3, T - S + PIECE, T)
-        load_w1(0, 0, PART)
-        load_w1(0, PART, HALF)
-        load_w1(1, 0, PART)
-        load_w1(1, PART, HALF)
-        load_w2(0, 0, PART)
-        load_w2(1, 0, PART)
-        load_w2(0, PART, N)
-        load_w2(1, PART, N)
-
-        h_codes = [
-            held.tile([P, S], U32, name="h_codes0", tag=f"raw_w1_1_{PART}", align_bytes=64),
-            words(S, "h_codes1"),
-        ]
+        for g in range(HALVES):
+            nc.sync.dma_start(w1_raw[g][:], w1_rows[:, :, HALF * g : HALF * (g + 1)])
+        nc.sync.dma_start(w2_first[:], w2_rows[0])
+        for a in range(N // PART):
+            nc.sync.dma_start(w2_second[a][:], w2_rows[1][:, :, PART * a : PART * (a + 1)])
 
         warm_in = held.tile([P, 1], F32, name="warm_in")
         warm_out = held.tile([P, 1], F32, name="warm_out")
@@ -103,155 +97,177 @@ def tile_picked_pick_mlp_relu_srt_e_kernel(tc, xT, w1, w2, offs, out):
             else:
                 nc.vector.tensor_copy(dst, src)
 
-        def quantise(codes, scales, values, lo, hi):
-            nc.vector.quantize_mx(
-                out=codes[:, lo:hi].bitcast(FP8X4), scales=scales[:, lo:hi], in_=values[:, PACK * lo : PACK * hi]
-            )
+        def quantise(codes, scales, values):
+            nc.vector.quantize_mx(out=codes.bitcast(FP8X4), scales=scales, in_=values)
 
         def gather(j, lo, hi):
             nc.vector.tensor_copy(
                 picked[:, j, lo:hi], planes[j][:, : T - S + hi].indirect(offsets[:, lo // 16 : hi // 16])
             )
 
-        def interleave(engine, dst, src):
-            copy(
-                engine,
-                dst.rearrange("p (q c j) -> p q j c", c=RUN, j=PACK),
-                src.rearrange("p j (q c) -> p q j c", c=RUN),
-            )
+        def cast_x(engine, u, s):
+            dst = x_bf[s][:].rearrange("p (q c u e) -> p u q e c", c=RUN, u=PAIR, e=PAIR)[:, u]
+            src = picked[:, PAIR * u : PAIR * (u + 1), PIECE * s : PIECE * (s + 1)]
+            copy(engine, dst, src.rearrange("p e (q c) -> p q e c", c=RUN))
 
-        def cast_x(engine, lo, hi):
-            interleave(engine, x_bf[:, PACK * lo : PACK * hi], picked[:, :, lo:hi])
+        def quantise_x(lo, hi, behind_w1):
+            if behind_w1:
+                codes = shared.tile([P, hi - lo], U32, name=f"x_codes{lo}", align_bytes=64, offset=4 * (lo - BLOCK))
+            else:
+                codes = words(hi - lo, f"x_codes{lo}")
+            for b in range(lo, hi, BLOCK):
+                x_codes[b] = codes[:, b - lo : b - lo + BLOCK]
+            first = PACK * (lo % PIECE)
+            quantise(codes[:], x_scales[:, lo:hi], x_bf[lo // PIECE][:, first : first + PACK * (hi - lo)])
 
-        def quantise_x(lo, hi):
-            x_codes[lo] = held.tile([P, hi - lo], U32, name=f"x_codes{lo}", tag=f"raw_w1_0_{lo}", align_bytes=64)
-            nc.vector.quantize_mx(
-                out=x_codes[lo][:].bitcast(FP8X4), scales=x_scales[:, lo:hi], in_=x_bf[:, PACK * lo : PACK * hi]
-            )
+        def cast_w1(engine, g, u, lo, hi, offset=None):
+            name = f"w1_bf{g}{u}{lo}"
+            if offset is None:
+                values = bf16_values(PAIR * (hi - lo), name)
+            else:
+                values = shared.tile([P, PACK * PAIR * (hi - lo)], BF16, name=name, align_bytes=64, offset=offset)
+            w1_bf[g, u, lo] = values
+            src = w1_raw[g][:].rearrange("p j (m u e) -> p u m j e", u=PAIR, e=PAIR)[:, u]
+            copy(engine, values[:].rearrange("p (e m j) -> p m j e", e=PAIR, j=PACK), src[:, lo:hi])
 
-        def cast_w1(engine, g, base, lo, hi):
-            dst = w1_bf[g][:].rearrange("p (t m j) -> p m j t", t=PACK, j=PACK)
-            src = raw["w1", g, base][:].rearrange("p j (m t) -> p m j t", t=PACK)
-            copy(engine, dst[:, lo // PACK : hi // PACK], src[:, (lo - base) // PACK : (hi - base) // PACK])
+        def quantise_w1(g, u):
+            columns = slice(PAIR * P * u, PAIR * P * (u + 1))
+            quantise(w1_codes[g][:, columns], w1_scales[g][:, columns], w1_bf[g, u, 0][:])
 
-        def quantise_w1(g, lo, hi):
-            quantise(w1_codes[g], w1_scales[g], w1_bf[g], lo, hi)
+        def quantise_w1_part(g, u, e, lo, hi):
+            first = P * (PAIR * u + e)
+            columns = slice(first + lo, first + hi)
+            values = w1_bf[g, u, lo][:, PACK * (hi - lo) * e : PACK * (hi - lo) * (e + 1)]
+            quantise(w1_codes[g][:, columns], w1_scales[g][:, columns], values)
 
-        def cast_w2(engine, g, base, lo, hi):
-            interleave(engine, w2_bf[g][:, PACK * lo : PACK * hi], raw["w2", g, base][:, :, lo - base : hi - base])
+        def cast_w2(engine, g, lo, hi, tag=None):
+            src = w2_first[:, :, lo:hi] if g == 0 else w2_second[lo // PART][:, :, lo % PART : lo % PART + hi - lo]
+            w2_bf[g, lo] = bf16_values(hi - lo, f"w2_bf{g}_{lo}", tag)
+            dst = w2_bf[g, lo][:].rearrange("p (q c j) -> p q j c", c=RUN, j=PACK)
+            copy(engine, dst, src.rearrange("p j (q c) -> p q j c", c=RUN))
 
         def quantise_w2(g, lo, hi):
-            quantise(w2_codes[g], w2_scales[g], w2_bf[g], lo, hi)
+            quantise(w2_codes[g][:, lo:hi], w2_scales[g][:, lo:hi], w2_bf[g, lo][:])
 
-        def layer1_block(engine, g, lo):
-            bank = psum.tile([P, PACK, BLOCK], F32, name="bank")
+        layer1_count = []
+
+        def layer1_block(g, lo):
+            number = len(layer1_count) % LAYER1_BANKS
+            layer1_count.append(lo)
+            bank = psum.tile([P, PACK, BLOCK], F32, name=f"hidden{g}_{lo}", offset=BANK_BYTES * number)
             tokens = slice(lo, lo + BLOCK)
-            base = min(lo // PIECE, 1) * PIECE
             for t in range(PACK):
                 channels = slice(P * t, P * (t + 1))
                 nc.tensor.matmul_mx(
                     out=bank[:, t, :],
                     lhsT=w1_codes[g][:, channels].bitcast(FP8X4),
                     lhsT_scale=w1_scales[g][:, channels],
-                    rhs=x_codes[base][:, lo - base : lo - base + BLOCK].bitcast(FP8X4),
+                    rhs=x_codes[lo].bitcast(FP8X4),
                     rhs_scale=x_scales[:, tokens],
                     start=True,
                     stop=True,
                 )
-            dst = h_bf[g][:, PACK * lo : PACK * (lo + BLOCK)].rearrange("p (n t) -> p n t", t=PACK)
-            src = bank[:].rearrange("p t n -> p n t")
-            if engine == "scalar":
-                nc.scalar.activation(dst, src, RELU)
+            first = PACK * (lo % PIECE)
+            dst = h_bf[g][lo // PIECE][:, first : first + PACK * BLOCK].rearrange("p (n t) -> p n t", t=PACK)
+            nc.scalar.activation(dst, bank[:].rearrange("p t n -> p n t"), RELU)
+
+        def quantise_h(g, s, tag=None):
+            tokens = slice(PIECE * s, PIECE * (s + 1))
+            h_codes[g, s] = words(PIECE, f"h_codes{g}{s}", tag)
+            quantise(h_codes[g, s][:], h_scales[g][:, tokens], h_bf[g][s][:])
+
+        banks = {}
+
+        def layer2_pass(g, number, parts):
+            if g == 0:
+                banks[parts] = psum.tile(
+                    [P, len(parts), PIECE], F32, name=f"sum{parts[0][0]}{parts[0][1]}", offset=BANK_BYTES * number
+                )
+            for d, (m, s) in enumerate(parts):
+                rows = slice(P * m, P * (m + 1))
+                nc.tensor.matmul_mx(
+                    out=banks[parts][:, d, :],
+                    lhsT=w2_codes[g][:, rows].bitcast(FP8X4),
+                    lhsT_scale=w2_scales[g][:, rows],
+                    rhs=h_codes[g, s][:].bitcast(FP8X4),
+                    rhs_scale=h_scales[g][:, PIECE * s : PIECE * (s + 1)],
+                    start=(g == 0 and d == 0),
+                    stop=(g == HALVES - 1 and d == len(parts) - 1),
+                )
+
+        def store(engine, parts):
+            (m, s), (last_m, last_s) = parts[0], parts[-1]
+            result = held.tile([P, len(parts), PIECE], F32, name=f"result{m}{s}")
+            copy(engine, result[:], banks[parts][:])
+            rows = out[P * m : P * (last_m + 1), PIECE * s : PIECE * (last_s + 1)]
+            if last_m > m:
+                nc.sync.dma_start(rows.rearrange("(d p) n -> p d n", d=len(parts)), result[:])
             else:
-                nc.vector.tensor_scalar_max(dst, src, 0.0)
+                nc.sync.dma_start(rows, result[:].rearrange("p d n -> p (d n)"))
 
-        def layer1(engine, g, s):
-            for lo in range(PIECE * s, PIECE * (s + 1), BLOCK):
-                layer1_block(engine, g, lo)
-
-        def quantise_h(g, lo, hi):
-            quantise(h_codes[g], h_scales[g], h_bf[g], lo, hi)
-
-        def layer2_pass(dst, g, m, lo, hi):
-            rows = slice(P * m, P * (m + 1))
-            nc.tensor.matmul_mx(
-                out=dst,
-                lhsT=w2_codes[g][:, rows].bitcast(FP8X4),
-                lhsT_scale=w2_scales[g][:, rows],
-                rhs=h_codes[g][:, lo:hi].bitcast(FP8X4),
-                rhs_scale=h_scales[g][:, lo:hi],
-                start=(g == 0),
-                stop=(g == HALVES - 1),
-            )
-
-        open_banks = {}
-
-        def first_pass(m, lo, hi):
-            open_banks[m, lo] = psum.tile([P, hi - lo], F32, name="bank")
-            layer2_pass(open_banks[m, lo][:], 0, m, lo, hi)
-
-        def last_pass(engine, m, lo, hi):
-            bank = open_banks[m, lo]
-            layer2_pass(bank[:], 1, m, lo, hi)
-            result = held.tile([P, hi - lo], F32, name=f"result{m}_{lo}")
-            copy(engine, result[:], bank[:])
-            nc.sync.dma_start(out[P * m : P * (m + 1), lo:hi], result[:])
-
-        def layer2_pair(engine, m0, lo, hi):
-            bank = psum.tile([P, 2, hi - lo], F32, name="bank")
-            for d in range(2):
-                for g in range(HALVES):
-                    layer2_pass(bank[:, d, :], g, m0 + d, lo, hi)
-            result = held.tile([P, 2, hi - lo], F32, name=f"pair{m0}_{lo}")
-            copy(engine, result[:], bank[:])
-            rows = out[P * m0 : P * (m0 + 2), lo:hi].rearrange("(d p) n -> p d n", d=2)
-            nc.sync.dma_start(rows, result[:])
-
-        for j in range(PACK - 1):
-            gather(j, 0, S)
+        gather(0, 0, S)
+        gather(1, 0, S)
+        for s in range(PIECES):
+            cast_x("scalar", 0, s)
+        gather(2, 0, S)
         for s in range(PIECES):
             gather(PACK - 1, PIECE * s, PIECE * (s + 1))
-        cast_x("scalar", 0, PIECE)
-        cast_w1("vector", 0, 0, 0, PART)
-        quantise_x(0, PIECE)
-        cast_x("scalar", PIECE, WIDE)
-        cast_w1("vector", 0, PART, PART, HALF)
-        quantise_w1(0, 0, PART)
-        quantise_w1(0, PART, HALF)
-        cast_x("scalar", WIDE, S)
-        quantise_x(PIECE, S)
-        cast_w1("scalar", 1, 0, 0, 192)
-        layer1("scalar", 0, 0)
-        cast_w1("vector", 1, 0, 192, PART)
-        layer1("scalar", 0, 1)
-        cast_w1("vector", 1, PART, PART, HALF)
-        quantise_w1(1, 0, PART)
-        quantise_w1(1, PART, HALF)
-        layer1("scalar", 1, 0)
-        layer1("scalar", 1, 1)
-        cast_w2("vector", 0, 0, 0, PART)
-        quantise_h(0, 0, PIECE)
-        cast_w2("vector", 1, 0, 0, PART)
+        cast_x("scalar", 1, 0)
+        cast_x("scalar", 1, 1)
+        cast_x("vector", 1, 2)
+        quantise_x(0, BLOCK, False)
+        quantise_x(WIDE, S, False)
+        cast_w1("vector", 0, 0, 0, P, 0)
+        cast_w1("scalar", 0, 1, SHARE, P)
+        cast_w1("vector", 0, 1, 0, SHARE)
+        quantise_w1(0, 0)
+        for e in range(PAIR):
+            quantise_w1_part(0, 1, e, 0, SHARE)
+            quantise_w1_part(0, 1, e, SHARE, P)
+        quantise_x(BLOCK, PIECE, True)
+        quantise_x(PIECE, WIDE, True)
+        top = [((0, s), (1, s)) for s in range(PIECES)]
+        wide = {m: ((m, 0), (m, 1)) for m in (2, 3)}
+        last = ((2, 2), (3, 2))
+        for lo in range(0, S, BLOCK):
+            layer1_block(0, lo)
+        cast_w1("vector", 1, 0, 0, P)
+        cast_w1("vector", 1, 1, 0, P)
+        quantise_w1(1, 0)
+        quantise_w1(1, 1)
+        for lo in range(0, S, BLOCK):
+            layer1_block(1, lo)
+        quantise_h(0, 0)
+        cast_w2("vector", 0, 0, PART)
+        cast_w2("vector", 0, PART, N)
         quantise_w2(0, 0, PART)
-        quantise_h(1, 0, PIECE)
+        cast_w2("vector", 1, 0, PART)
+        quantise_h(0, 1, "w2_first")
+        quantise_h(1, 0)
         quantise_w2(1, 0, PART)
-        quantise_h(0, PIECE, WIDE)
-        layer2_pair("scalar", 0, 0, PIECE)
-        layer1("scalar", 0, 2)
-        layer1("scalar", 1, 2)
-        cast_w2("vector", 0, PART, PART, N)
-        quantise_h(1, PIECE, WIDE)
+        for g in range(HALVES):
+            layer2_pass(g, 4, top[0])
+        store("scalar", top[0])
         quantise_w2(0, PART, N)
-        for m in (2, 3):
-            first_pass(m, 0, WIDE)
-        cast_w2("vector", 1, PART, PART, N)
-        quantise_h(0, WIDE, S)
-        quantise_w2(1, PART, N)
-        layer2_pair("vector", 0, PIECE, WIDE)
-        last_pass("scalar", 2, 0, WIDE)
-        quantise_h(1, WIDE, S)
-        last_pass("scalar", 3, 0, WIDE)
-        for m in range(4):
-            first_pass(m, WIDE, S)
-        for m in range(4):
-            last_pass("scalar" if m % 2 else "vector", m, WIDE, S)
+        cast_w2("vector", 1, 2 * P, 3 * P)
+        quantise_h(1, 1)
+        for g in range(HALVES):
+            layer2_pass(g, 5, top[1])
+        quantise_w2(1, 2 * P, 3 * P)
+        for g in range(HALVES):
+            layer2_pass(g, 7, wide[2])
+        quantise_h(0, 2, "w2_second0")
+        layer2_pass(0, 1, wide[3])
+        layer2_pass(0, 6, top[2])
+        layer2_pass(0, 0, last)
+        store("scalar", top[1])
+        store("scalar", wide[2])
+        cast_w2("vector", 1, 3 * P, N)
+        quantise_h(1, 2)
+        layer2_pass(1, 6, top[2])
+        quantise_w2(1, 3 * P, N)
+        layer2_pass(1, 1, wide[3])
+        layer2_pass(1, 0, last)
+        store("vector", top[2])
+        store("scalar", wide[3])
+        store("vector", last)

@@ -18,7 +18,7 @@ PAIR = 2
 BANK_BYTES = 2048
 LAYER1_BANKS = 4
 SHARE = 64
-RUN = 4
+RUN = 2
 
 F32 = mybir.dt.float32
 BF16 = mybir.dt.bfloat16
@@ -37,19 +37,19 @@ def tile_picked_pick_mlp_relu_srt_e_kernel(tc, xT, w1, w2, offs, out):
         psum = ctx.enter_context(tc.psum_pool(name="psum", bufs=1))
 
         def words(width, name, tag=None):
-            return held.tile([P, width], U32, name=name, tag=tag or name, align_bytes=64)
+            return held.tile([P, width], U32, name=name, tag=tag or name, align_bytes=256)
 
         def scale_bytes(width, name):
             return held.tile([P, width], U8, name=name, align_bytes=64)
 
         def bf16_values(width, name, tag=None):
-            return held.tile([P, PACK * width], BF16, name=name, tag=tag or name, align_bytes=64)
+            return held.tile([P, PACK * width], BF16, name=name, tag=tag or name, align_bytes=256)
 
         def raw_rows(width, name):
-            return held.tile([P, PACK, width], F32, name=name, align_bytes=64)
+            return held.tile([P, PACK, width], F32, name=name, align_bytes=256)
 
         offsets = held.tile([P, S // 16], U16, name="offsets")
-        planes = [held.tile([P, T], F32, name=f"plane{j}", align_bytes=64) for j in range(PACK)]
+        planes = [held.tile([P, T], F32, name=f"plane{j}", align_bytes=256) for j in range(PACK)]
         picked = raw_rows(S, "picked")
         x_bf = [bf16_values(PIECE, f"x_bf{s}") for s in range(PIECES)]
         x_codes = {}
@@ -197,7 +197,7 @@ def tile_picked_pick_mlp_relu_srt_e_kernel(tc, xT, w1, w2, offs, out):
 
         def store(engine, parts):
             (m, s), (last_m, last_s) = parts[0], parts[-1]
-            result = held.tile([P, len(parts), PIECE], F32, name=f"result{m}{s}")
+            result = held.tile([P, len(parts), PIECE], F32, name=f"result{m}{s}", align_bytes=256)
             copy(engine, result[:], banks[parts][:])
             rows = out[P * m : P * (last_m + 1), PIECE * s : PIECE * (last_s + 1)]
             if last_m > m:
@@ -235,7 +235,7 @@ def tile_picked_pick_mlp_relu_srt_e_kernel(tc, xT, w1, w2, offs, out):
         cast_w1("vector", 1, 1, 0, P)
         quantise_w1(1, 0)
         quantise_w1(1, 1)
-        for lo in range(0, S, BLOCK):
+        for lo in range(0, S - BLOCK, BLOCK):
             layer1_block(1, lo)
         quantise_h(0, 0)
         cast_w2("vector", 0, 0, PART)
@@ -248,6 +248,7 @@ def tile_picked_pick_mlp_relu_srt_e_kernel(tc, xT, w1, w2, offs, out):
         for g in range(HALVES):
             layer2_pass(g, 4, top[0])
         store("scalar", top[0])
+        layer1_block(1, S - BLOCK)
         quantise_w2(0, PART, N)
         cast_w2("vector", 1, 2 * P, 3 * P)
         quantise_h(1, 1)
@@ -261,13 +262,13 @@ def tile_picked_pick_mlp_relu_srt_e_kernel(tc, xT, w1, w2, offs, out):
         layer2_pass(0, 6, top[2])
         layer2_pass(0, 0, last)
         store("scalar", top[1])
-        store("scalar", wide[2])
         cast_w2("vector", 1, 3 * P, N)
-        quantise_h(1, 2)
-        layer2_pass(1, 6, top[2])
         quantise_w2(1, 3 * P, N)
         layer2_pass(1, 1, wide[3])
+        quantise_h(1, 2)
+        layer2_pass(1, 6, top[2])
         layer2_pass(1, 0, last)
-        store("vector", top[2])
-        store("scalar", wide[3])
+        store("scalar", wide[2])
+        store("vector", wide[3])
+        store("scalar", top[2])
         store("vector", last)

@@ -40,7 +40,7 @@ def tile_picked_pick_mlp_relu_srt_e_kernel(tc, xT, w1, w2, offs, out):
             return held.tile([P, width], U32, name=name, tag=tag or name, align_bytes=256)
 
         def scale_bytes(width, name):
-            return held.tile([P, width], U8, name=name, align_bytes=64)
+            return held.tile([P, width], U8, name=name, align_bytes=256)
 
         def bf16_values(width, name, tag=None):
             return held.tile([P, PACK * width], BF16, name=name, tag=tag or name, align_bytes=256)
@@ -70,6 +70,7 @@ def tile_picked_pick_mlp_relu_srt_e_kernel(tc, xT, w1, w2, offs, out):
         x_rows = xT.rearrange("(p j) w -> p j w", j=PACK)
         w1_rows = w1.rearrange("(p j) i -> p j i", j=PACK)
         w2_rows = w2.rearrange("(g p j) m -> g p j m", g=HALVES, j=PACK)
+        w2_pairs = w2.rearrange("(g u a c b) m -> g a u c (b m)", g=HALVES, a=PAIR, c=PAIR, b=PAIR)
 
         def load_plane(j, lo, hi):
             nc.sync.dma_start(planes[j][:, lo:hi], x_rows[:, j, lo:hi])
@@ -82,9 +83,11 @@ def tile_picked_pick_mlp_relu_srt_e_kernel(tc, xT, w1, w2, offs, out):
         load_plane(3, T - S + PIECE, T)
         for g in range(HALVES):
             nc.sync.dma_start(w1_raw[g][:], w1_rows[:, :, HALF * g : HALF * (g + 1)])
-        nc.sync.dma_start(w2_first[:], w2_rows[0])
+        for a in range(PAIR):
+            slots = w2_first[:, PAIR * a : PAIR * (a + 1), :].rearrange("p b m -> p (b m)")
+            nc.sync.dma_start(slots, w2_pairs[1, a])
         for a in range(N // PART):
-            nc.sync.dma_start(w2_second[a][:], w2_rows[1][:, :, PART * a : PART * (a + 1)])
+            nc.sync.dma_start(w2_second[a][:], w2_rows[0][:, :, PART * a : PART * (a + 1)])
 
         warm_in = held.tile([P, 1], F32, name="warm_in")
         warm_out = held.tile([P, 1], F32, name="warm_out")
@@ -110,9 +113,14 @@ def tile_picked_pick_mlp_relu_srt_e_kernel(tc, xT, w1, w2, offs, out):
             src = picked[:, PAIR * u : PAIR * (u + 1), PIECE * s : PIECE * (s + 1)]
             copy(engine, dst, src.rearrange("p e (q c) -> p q e c", c=RUN))
 
+        def cast_x_whole(s):
+            dst = x_bf[s][:].rearrange("p (q c j) -> p q j c", c=RUN, j=PACK)
+            src = picked[:, :, PIECE * s : PIECE * (s + 1)]
+            nc.vector.tensor_copy(dst, src.rearrange("p j (q c) -> p q j c", c=RUN))
+
         def quantise_x(lo, hi, behind_w1):
             if behind_w1:
-                codes = shared.tile([P, hi - lo], U32, name=f"x_codes{lo}", align_bytes=64, offset=4 * (lo - BLOCK))
+                codes = shared.tile([P, hi - lo], U32, name=f"x_codes{lo}", align_bytes=256, offset=4 * (lo - BLOCK))
             else:
                 codes = words(hi - lo, f"x_codes{lo}")
             for b in range(lo, hi, BLOCK):
@@ -125,10 +133,15 @@ def tile_picked_pick_mlp_relu_srt_e_kernel(tc, xT, w1, w2, offs, out):
             if offset is None:
                 values = bf16_values(PAIR * (hi - lo), name)
             else:
-                values = shared.tile([P, PACK * PAIR * (hi - lo)], BF16, name=name, align_bytes=64, offset=offset)
+                values = shared.tile([P, PACK * PAIR * (hi - lo)], BF16, name=name, align_bytes=256, offset=offset)
             w1_bf[g, u, lo] = values
-            src = w1_raw[g][:].rearrange("p j (m u e) -> p u m j e", u=PAIR, e=PAIR)[:, u]
-            copy(engine, values[:].rearrange("p (e m j) -> p m j e", e=PAIR, j=PACK), src[:, lo:hi])
+            if g == 0:
+                src = w1_raw[g][:].rearrange("p j (m u e) -> p u m j e", u=PAIR, e=PAIR)[:, u]
+                copy(engine, values[:].rearrange("p (e m j) -> p m j e", e=PAIR, j=PACK), src[:, lo:hi])
+            else:
+                src = w1_raw[g][:].rearrange("p j (v a c b) -> p a v b j c", a=PAIR, c=PAIR, b=PAIR)[:, u]
+                dst = values[:].rearrange("p (b v c j) -> p v b j c", b=PAIR, c=PAIR, j=PACK)
+                copy(engine, dst, src[:, lo // PAIR : hi // PAIR])
 
         def quantise_w1(g, u):
             columns = slice(PAIR * P * u, PAIR * P * (u + 1))
@@ -141,7 +154,7 @@ def tile_picked_pick_mlp_relu_srt_e_kernel(tc, xT, w1, w2, offs, out):
             quantise(w1_codes[g][:, columns], w1_scales[g][:, columns], values)
 
         def cast_w2(engine, g, lo, hi, tag=None):
-            src = w2_first[:, :, lo:hi] if g == 0 else w2_second[lo // PART][:, :, lo % PART : lo % PART + hi - lo]
+            src = w2_first[:, :, lo:hi] if g == 1 else w2_second[lo // PART][:, :, lo % PART : lo % PART + hi - lo]
             w2_bf[g, lo] = bf16_values(hi - lo, f"w2_bf{g}_{lo}", tag)
             dst = w2_bf[g, lo][:].rearrange("p (q c j) -> p q j c", c=RUN, j=PACK)
             copy(engine, dst, src.rearrange("p j (q c) -> p q j c", c=RUN))
@@ -151,8 +164,8 @@ def tile_picked_pick_mlp_relu_srt_e_kernel(tc, xT, w1, w2, offs, out):
 
         layer1_count = []
 
-        def layer1_block(g, lo):
-            number = len(layer1_count) % LAYER1_BANKS
+        def layer1_block(g, lo, back=0):
+            number = (len(layer1_count) - back) % LAYER1_BANKS
             layer1_count.append(lo)
             bank = psum.tile([P, PACK, BLOCK], F32, name=f"hidden{g}_{lo}", offset=BANK_BYTES * number)
             tokens = slice(lo, lo + BLOCK)
@@ -178,8 +191,8 @@ def tile_picked_pick_mlp_relu_srt_e_kernel(tc, xT, w1, w2, offs, out):
 
         banks = {}
 
-        def layer2_pass(g, number, parts):
-            if g == 0:
+        def layer2_pass(g, number, parts, opens):
+            if opens:
                 banks[parts] = psum.tile(
                     [P, len(parts), PIECE], F32, name=f"sum{parts[0][0]}{parts[0][1]}", offset=BANK_BYTES * number
                 )
@@ -191,8 +204,8 @@ def tile_picked_pick_mlp_relu_srt_e_kernel(tc, xT, w1, w2, offs, out):
                     lhsT_scale=w2_scales[g][:, rows],
                     rhs=h_codes[g, s][:].bitcast(FP8X4),
                     rhs_scale=h_scales[g][:, PIECE * s : PIECE * (s + 1)],
-                    start=(g == 0 and d == 0),
-                    stop=(g == HALVES - 1 and d == len(parts) - 1),
+                    start=(opens and d == 0),
+                    stop=(not opens and d == len(parts) - 1),
                 )
 
         def store(engine, parts):
@@ -207,16 +220,15 @@ def tile_picked_pick_mlp_relu_srt_e_kernel(tc, xT, w1, w2, offs, out):
 
         gather(0, 0, S)
         gather(1, 0, S)
-        for s in range(PIECES):
+        for s in range(PIECES - 1):
             cast_x("scalar", 0, s)
         gather(2, 0, S)
         for s in range(PIECES):
             gather(PACK - 1, PIECE * s, PIECE * (s + 1))
         cast_x("scalar", 1, 0)
         cast_x("scalar", 1, 1)
-        cast_x("vector", 1, 2)
         quantise_x(0, BLOCK, False)
-        quantise_x(WIDE, S, False)
+        cast_x_whole(2)
         cast_w1("vector", 0, 0, 0, P, 0)
         cast_w1("scalar", 0, 1, SHARE, P)
         cast_w1("vector", 0, 1, 0, SHARE)
@@ -226,6 +238,7 @@ def tile_picked_pick_mlp_relu_srt_e_kernel(tc, xT, w1, w2, offs, out):
             quantise_w1_part(0, 1, e, SHARE, P)
         quantise_x(BLOCK, PIECE, True)
         quantise_x(PIECE, WIDE, True)
+        quantise_x(WIDE, S, True)
         top = [((0, s), (1, s)) for s in range(PIECES)]
         wide = {m: ((m, 0), (m, 1)) for m in (2, 3)}
         last = ((2, 2), (3, 2))
@@ -235,40 +248,39 @@ def tile_picked_pick_mlp_relu_srt_e_kernel(tc, xT, w1, w2, offs, out):
         cast_w1("vector", 1, 1, 0, P)
         quantise_w1(1, 0)
         quantise_w1(1, 1)
-        for lo in range(0, S - BLOCK, BLOCK):
+        for lo in range(0, S, BLOCK):
             layer1_block(1, lo)
         quantise_h(0, 0)
-        cast_w2("vector", 0, 0, PART)
-        cast_w2("vector", 0, PART, N)
-        quantise_w2(0, 0, PART)
         cast_w2("vector", 1, 0, PART)
+        cast_w2("vector", 1, PART, N)
+        quantise_w2(1, 0, PART)
+        cast_w2("vector", 0, 0, PART)
         quantise_h(0, 1, "w2_first")
         quantise_h(1, 0)
-        quantise_w2(1, 0, PART)
-        for g in range(HALVES):
-            layer2_pass(g, 4, top[0])
+        layer2_pass(1, 4, top[0], True)
+        quantise_w2(0, 0, PART)
+        layer2_pass(0, 4, top[0], False)
         store("scalar", top[0])
-        layer1_block(1, S - BLOCK)
-        quantise_w2(0, PART, N)
-        cast_w2("vector", 1, 2 * P, 3 * P)
+        layer2_pass(0, 5, top[1], True)
+        quantise_w2(1, PART, N)
+        cast_w2("vector", 0, 2 * P, 3 * P)
         quantise_h(1, 1)
-        for g in range(HALVES):
-            layer2_pass(g, 5, top[1])
-        quantise_w2(1, 2 * P, 3 * P)
-        for g in range(HALVES):
-            layer2_pass(g, 7, wide[2])
-        quantise_h(0, 2, "w2_second0")
-        layer2_pass(0, 1, wide[3])
-        layer2_pass(0, 6, top[2])
-        layer2_pass(0, 0, last)
+        layer2_pass(1, 5, top[1], False)
         store("scalar", top[1])
-        cast_w2("vector", 1, 3 * P, N)
-        quantise_w2(1, 3 * P, N)
-        layer2_pass(1, 1, wide[3])
-        quantise_h(1, 2)
-        layer2_pass(1, 6, top[2])
-        layer2_pass(1, 0, last)
+        layer2_pass(1, 7, wide[2], True)
+        quantise_w2(0, 2 * P, 3 * P)
+        layer2_pass(0, 7, wide[2], False)
         store("scalar", wide[2])
-        store("vector", wide[3])
-        store("scalar", top[2])
+        layer2_pass(1, 1, wide[3], True)
+        quantise_h(0, 2, "w2_second0")
+        layer2_pass(0, 6, top[2], True)
+        cast_w2("vector", 0, 3 * P, N)
+        quantise_h(1, 2)
+        layer2_pass(1, 6, top[2], False)
+        layer2_pass(1, 0, last, True)
+        quantise_w2(0, 3 * P, N)
+        layer2_pass(0, 1, wide[3], False)
+        layer2_pass(0, 0, last, False)
+        store("vector", top[2])
+        store("scalar", wide[3])
         store("vector", last)

@@ -85,9 +85,9 @@ def tile_picked_pick_mlp_relu_srt_e_kernel(tc, xT, w1, w2, offs, out):
             nc.sync.dma_start(w1_raw[g][:], w1_rows[:, :, HALF * g : HALF * (g + 1)])
         for a in range(PAIR):
             slots = w2_first[:, PAIR * a : PAIR * (a + 1), :].rearrange("p b m -> p (b m)")
-            nc.sync.dma_start(slots, w2_pairs[1, a])
+            nc.sync.dma_start(slots, w2_pairs[0, a])
         for a in range(N // PART):
-            nc.sync.dma_start(w2_second[a][:], w2_rows[0][:, :, PART * a : PART * (a + 1)])
+            nc.sync.dma_start(w2_second[a][:], w2_rows[1][:, :, PART * a : PART * (a + 1)])
 
         warm_in = held.tile([P, 1], F32, name="warm_in")
         warm_out = held.tile([P, 1], F32, name="warm_out")
@@ -135,7 +135,7 @@ def tile_picked_pick_mlp_relu_srt_e_kernel(tc, xT, w1, w2, offs, out):
             else:
                 values = shared.tile([P, PACK * PAIR * (hi - lo)], BF16, name=name, align_bytes=256, offset=offset)
             w1_bf[g, u, lo] = values
-            if g == 0:
+            if g == 1:
                 src = w1_raw[g][:].rearrange("p j (m u e) -> p u m j e", u=PAIR, e=PAIR)[:, u]
                 copy(engine, values[:].rearrange("p (e m j) -> p m j e", e=PAIR, j=PACK), src[:, lo:hi])
             else:
@@ -154,7 +154,7 @@ def tile_picked_pick_mlp_relu_srt_e_kernel(tc, xT, w1, w2, offs, out):
             quantise(w1_codes[g][:, columns], w1_scales[g][:, columns], values)
 
         def cast_w2(engine, g, lo, hi, tag=None):
-            src = w2_first[:, :, lo:hi] if g == 1 else w2_second[lo // PART][:, :, lo % PART : lo % PART + hi - lo]
+            src = w2_first[:, :, lo:hi] if g == 0 else w2_second[lo // PART][:, :, lo % PART : lo % PART + hi - lo]
             w2_bf[g, lo] = bf16_values(hi - lo, f"w2_bf{g}_{lo}", tag)
             dst = w2_bf[g, lo][:].rearrange("p (q c j) -> p q j c", c=RUN, j=PACK)
             copy(engine, dst, src.rearrange("p j (q c) -> p q j c", c=RUN))
@@ -241,7 +241,7 @@ def tile_picked_pick_mlp_relu_srt_e_kernel(tc, xT, w1, w2, offs, out):
         quantise_x(WIDE, S, True)
         top = [((0, s), (1, s)) for s in range(PIECES)]
         wide = {m: ((m, 0), (m, 1)) for m in (2, 3)}
-        last = ((2, 2), (3, 2))
+        last = {m: ((m, 2),) for m in (2, 3)}
         for lo in range(0, S, BLOCK):
             layer1_block(0, lo)
         cast_w1("vector", 1, 0, 0, P)
@@ -251,36 +251,39 @@ def tile_picked_pick_mlp_relu_srt_e_kernel(tc, xT, w1, w2, offs, out):
         for lo in range(0, S, BLOCK):
             layer1_block(1, lo)
         quantise_h(0, 0)
-        cast_w2("vector", 1, 0, PART)
-        cast_w2("vector", 1, PART, N)
-        quantise_w2(1, 0, PART)
         cast_w2("vector", 0, 0, PART)
-        quantise_h(0, 1, "w2_first")
-        quantise_h(1, 0)
-        layer2_pass(1, 4, top[0], True)
+        cast_w2("vector", 0, PART, N)
         quantise_w2(0, 0, PART)
-        layer2_pass(0, 4, top[0], False)
-        store("scalar", top[0])
+        layer2_pass(0, 4, top[0], True)
+        cast_w2("vector", 1, 0, PART)
+        quantise_h(0, 1, "w2_first")
         layer2_pass(0, 5, top[1], True)
-        quantise_w2(1, PART, N)
-        cast_w2("vector", 0, 2 * P, 3 * P)
+        quantise_h(1, 0)
+        quantise_w2(1, 0, PART)
+        layer2_pass(1, 4, top[0], False)
+        store("scalar", top[0])
+        quantise_w2(0, PART, N)
+        layer2_pass(0, 7, wide[2], True)
+        layer2_pass(0, 6, wide[3], True)
+        cast_w2("vector", 1, 2 * P, 3 * P)
         quantise_h(1, 1)
         layer2_pass(1, 5, top[1], False)
         store("scalar", top[1])
-        layer2_pass(1, 7, wide[2], True)
-        quantise_w2(0, 2 * P, 3 * P)
-        layer2_pass(0, 7, wide[2], False)
+        quantise_w2(1, 2 * P, 3 * P)
+        layer2_pass(1, 7, wide[2], False)
         store("scalar", wide[2])
-        layer2_pass(1, 1, wide[3], True)
         quantise_h(0, 2, "w2_second0")
-        layer2_pass(0, 6, top[2], True)
-        cast_w2("vector", 0, 3 * P, N)
+        layer2_pass(0, 0, last[2], True)
+        layer2_pass(0, 1, top[2], True)
+        layer2_pass(0, 2, last[3], True)
+        cast_w2("vector", 1, 3 * P, N)
         quantise_h(1, 2)
-        layer2_pass(1, 6, top[2], False)
-        layer2_pass(1, 0, last, True)
-        quantise_w2(0, 3 * P, N)
-        layer2_pass(0, 1, wide[3], False)
-        layer2_pass(0, 0, last, False)
+        layer2_pass(1, 0, last[2], False)
+        layer2_pass(1, 1, top[2], False)
+        quantise_w2(1, 3 * P, N)
+        layer2_pass(1, 6, wide[3], False)
+        layer2_pass(1, 2, last[3], False)
+        store("scalar", last[2])
         store("vector", top[2])
         store("scalar", wide[3])
-        store("vector", last)
+        store("vector", last[3])

@@ -16,7 +16,7 @@ PART = 256
 WIDE = 2 * PIECE
 PAIR = 2
 BANK_BYTES = 2048
-LAYER1_BANKS = 4
+BANKS = 8
 SHARE = 64
 RUN = 2
 
@@ -69,8 +69,7 @@ def tile_picked_pick_mlp_relu_srt_e_kernel(tc, xT, w1, w2, offs, out):
 
         x_rows = xT.rearrange("(p j) w -> p j w", j=PACK)
         w1_rows = w1.rearrange("(p j) i -> p j i", j=PACK)
-        w2_rows = w2.rearrange("(g p j) m -> g p j m", g=HALVES, j=PACK)
-        w2_pairs = w2.rearrange("(g u a c b) m -> g a u c (b m)", g=HALVES, a=PAIR, c=PAIR, b=PAIR)
+        w2_rows = w2.rearrange("(g u a r) m -> g a u r m", g=HALVES, a=PAIR, r=PACK)
 
         def load_plane(j, lo, hi):
             nc.sync.dma_start(planes[j][:, lo:hi], x_rows[:, j, lo:hi])
@@ -83,11 +82,15 @@ def tile_picked_pick_mlp_relu_srt_e_kernel(tc, xT, w1, w2, offs, out):
         load_plane(3, T - S + PIECE, T)
         for g in range(HALVES):
             nc.sync.dma_start(w1_raw[g][:], w1_rows[:, :, HALF * g : HALF * (g + 1)])
-        for a in range(PAIR):
-            slots = w2_first[:, PAIR * a : PAIR * (a + 1), :].rearrange("p b m -> p (b m)")
-            nc.sync.dma_start(slots, w2_pairs[0, a])
-        for a in range(N // PART):
-            nc.sync.dma_start(w2_second[a][:], w2_rows[1][:, :, PART * a : PART * (a + 1)])
+
+        def load_w2(raw, g, lo, hi):
+            for a in range(PAIR):
+                slots = raw[:, PAIR * a : PAIR * (a + 1), :].rearrange("p b m -> p (b m)")
+                nc.sync.dma_start(slots, w2_rows[g, a][:, :, lo:hi])
+
+        load_w2(w2_first, 0, 0, N)
+        for part in range(N // PART):
+            load_w2(w2_second[part], 1, PART * part, PART * (part + 1))
 
         warm_in = held.tile([P, 1], F32, name="warm_in")
         warm_out = held.tile([P, 1], F32, name="warm_out")
@@ -135,13 +138,9 @@ def tile_picked_pick_mlp_relu_srt_e_kernel(tc, xT, w1, w2, offs, out):
             else:
                 values = shared.tile([P, PACK * PAIR * (hi - lo)], BF16, name=name, align_bytes=256, offset=offset)
             w1_bf[g, u, lo] = values
-            if g == 1:
-                src = w1_raw[g][:].rearrange("p j (m u e) -> p u m j e", u=PAIR, e=PAIR)[:, u]
-                copy(engine, values[:].rearrange("p (e m j) -> p m j e", e=PAIR, j=PACK), src[:, lo:hi])
-            else:
-                src = w1_raw[g][:].rearrange("p j (v a c b) -> p a v b j c", a=PAIR, c=PAIR, b=PAIR)[:, u]
-                dst = values[:].rearrange("p (b v c j) -> p v b j c", b=PAIR, c=PAIR, j=PACK)
-                copy(engine, dst, src[:, lo // PAIR : hi // PAIR])
+            src = w1_raw[g][:].rearrange("p j (v a c b) -> p a v b j c", a=PAIR, c=PAIR, b=PAIR)[:, u]
+            dst = values[:].rearrange("p (b v c j) -> p v b j c", b=PAIR, c=PAIR, j=PACK)
+            copy(engine, dst, src[:, lo // PAIR : hi // PAIR])
 
         def quantise_w1(g, u):
             columns = slice(PAIR * P * u, PAIR * P * (u + 1))
@@ -162,11 +161,7 @@ def tile_picked_pick_mlp_relu_srt_e_kernel(tc, xT, w1, w2, offs, out):
         def quantise_w2(g, lo, hi):
             quantise(w2_codes[g][:, lo:hi], w2_scales[g][:, lo:hi], w2_bf[g, lo][:])
 
-        layer1_count = []
-
-        def layer1_block(g, lo, back=0):
-            number = (len(layer1_count) - back) % LAYER1_BANKS
-            layer1_count.append(lo)
+        def layer1_block(g, lo, number):
             bank = psum.tile([P, PACK, BLOCK], F32, name=f"hidden{g}_{lo}", offset=BANK_BYTES * number)
             tokens = slice(lo, lo + BLOCK)
             for t in range(PACK):
@@ -191,12 +186,14 @@ def tile_picked_pick_mlp_relu_srt_e_kernel(tc, xT, w1, w2, offs, out):
 
         banks = {}
 
-        def layer2_pass(g, number, parts, opens):
+        def layer2_pass(g, number, parts, opens, only=None):
             if opens:
                 banks[parts] = psum.tile(
                     [P, len(parts), PIECE], F32, name=f"sum{parts[0][0]}{parts[0][1]}", offset=BANK_BYTES * number
                 )
             for d, (m, s) in enumerate(parts):
+                if only is not None and d != only:
+                    continue
                 rows = slice(P * m, P * (m + 1))
                 nc.tensor.matmul_mx(
                     out=banks[parts][:, d, :],
@@ -207,6 +204,12 @@ def tile_picked_pick_mlp_relu_srt_e_kernel(tc, xT, w1, w2, offs, out):
                     start=(opens and d == 0),
                     stop=(not opens and d == len(parts) - 1),
                 )
+
+        def store_rows(m, first, second):
+            result = held.tile([P, PIECES, PIECE], F32, name=f"rows{m}", align_bytes=256)
+            copy(first, result[:, : PIECES - 1, :], banks[(m, 0), (m, 1)][:])
+            copy(second, result[:, PIECES - 1 :, :], banks[((m, 2),)][:])
+            nc.sync.dma_start(out[P * m : P * (m + 1), :], result[:].rearrange("p d n -> p (d n)"))
 
         def store(engine, parts):
             (m, s), (last_m, last_s) = parts[0], parts[-1]
@@ -239,51 +242,55 @@ def tile_picked_pick_mlp_relu_srt_e_kernel(tc, xT, w1, w2, offs, out):
         quantise_x(BLOCK, PIECE, True)
         quantise_x(PIECE, WIDE, True)
         quantise_x(WIDE, S, True)
-        top = [((0, s), (1, s)) for s in range(PIECES)]
-        wide = {m: ((m, 0), (m, 1)) for m in (2, 3)}
+        wide = [((m, 0), (m, 1)) for m in range(N // P)]
+        top = ((0, 2), (1, 2))
         last = {m: ((m, 2),) for m in (2, 3)}
-        for lo in range(0, S, BLOCK):
-            layer1_block(0, lo)
+        for b in range(5):
+            layer1_block(0, BLOCK * b, b)
         cast_w1("vector", 1, 0, 0, P)
         cast_w1("vector", 1, 1, 0, P)
         quantise_w1(1, 0)
         quantise_w1(1, 1)
-        for lo in range(0, S, BLOCK):
-            layer1_block(1, lo)
+        for b in range(4):
+            layer1_block(1, BLOCK * b, (5 + b) % BANKS)
+        layer1_block(0, S - BLOCK, 5)
+        for b in range(4, 6):
+            layer1_block(1, BLOCK * b, b - 3)
         quantise_h(0, 0)
         cast_w2("vector", 0, 0, PART)
         cast_w2("vector", 0, PART, N)
         quantise_w2(0, 0, PART)
-        layer2_pass(0, 4, top[0], True)
         cast_w2("vector", 1, 0, PART)
         quantise_h(0, 1, "w2_first")
-        layer2_pass(0, 5, top[1], True)
-        quantise_h(1, 0)
+        layer2_pass(0, 3, wide[0], True)
+        layer2_pass(0, 4, wide[1], True)
+        quantise_h(1, 0, "w2_second0")
         quantise_w2(1, 0, PART)
-        layer2_pass(1, 4, top[0], False)
-        store("scalar", top[0])
+        layer2_pass(1, 3, wide[0], False, 0)
+        layer2_pass(1, 4, wide[1], False, 0)
+        quantise_h(1, 1, "w2_bf0_0")
+        layer2_pass(1, 3, wide[0], False, 1)
+        layer2_pass(1, 4, wide[1], False, 1)
+        store("scalar", wide[0])
+        store("scalar", wide[1])
         quantise_w2(0, PART, N)
         layer2_pass(0, 7, wide[2], True)
         layer2_pass(0, 6, wide[3], True)
         cast_w2("vector", 1, 2 * P, 3 * P)
-        quantise_h(1, 1)
-        layer2_pass(1, 5, top[1], False)
-        store("scalar", top[1])
+        quantise_h(0, 2, "w2_bf1_0")
         quantise_w2(1, 2 * P, 3 * P)
         layer2_pass(1, 7, wide[2], False)
         store("scalar", wide[2])
-        quantise_h(0, 2, "w2_second0")
         layer2_pass(0, 0, last[2], True)
-        layer2_pass(0, 1, top[2], True)
-        layer2_pass(0, 2, last[3], True)
+        layer2_pass(0, 5, top, True)
+        layer2_pass(0, 1, last[3], True)
         cast_w2("vector", 1, 3 * P, N)
         quantise_h(1, 2)
         layer2_pass(1, 0, last[2], False)
-        layer2_pass(1, 1, top[2], False)
+        layer2_pass(1, 5, top, False)
         quantise_w2(1, 3 * P, N)
         layer2_pass(1, 6, wide[3], False)
-        layer2_pass(1, 2, last[3], False)
+        layer2_pass(1, 1, last[3], False)
         store("scalar", last[2])
-        store("vector", top[2])
-        store("scalar", wide[3])
-        store("vector", last[3])
+        store("vector", top)
+        store_rows(3, "scalar", "vector")

@@ -6,19 +6,21 @@ K, T, S, H, N = 512, 2048, 768, 1024, 512
 FLOPS = 2 * S * K * H + 2 * S * H * N
 
 P = 128
-PACK = 4
-HALF = P * PACK
+SLOTS = 4
+TWO = 2
+HALF = P * SLOTS
 HALVES = H // HALF
 PIECE = 256
 PIECES = S // PIECE
+LAST = PIECES - 1
 BLOCK = 128
+BLOCKS = S // BLOCK
 PART = 256
-WIDE = 2 * PIECE
-PAIR = 2
+SPLIT = 64
+RUN = 2
 BANK_BYTES = 2048
 BANKS = 8
-SHARE = 64
-RUN = 2
+ALIGN = 256
 
 F32 = mybir.dt.float32
 BF16 = mybir.dt.bfloat16
@@ -31,62 +33,62 @@ RELU = mybir.ActivationFunctionType.Relu
 
 def tile_picked_pick_mlp_relu_srt_e_kernel(tc, xT, w1, w2, offs, out):
     nc = tc.nc
+    on_vector, on_scalar = nc.vector.tensor_copy, nc.scalar.copy
     with ExitStack() as ctx:
         held = ctx.enter_context(tc.tile_pool(name="held", bufs=1))
-        shared = ctx.enter_context(tc.tile_pool(name="shared", bufs=1))
+        overlaid = ctx.enter_context(tc.tile_pool(name="overlaid", bufs=1))
         psum = ctx.enter_context(tc.psum_pool(name="psum", bufs=1))
 
-        def words(width, name, tag=None):
-            return held.tile([P, width], U32, name=name, tag=tag or name, align_bytes=256)
+        def words(width, name, after=None):
+            return held.tile([P, width], U32, name=name, tag=after or name, align_bytes=ALIGN)
 
         def scale_bytes(width, name):
-            return held.tile([P, width], U8, name=name, align_bytes=256)
+            return held.tile([P, width], U8, name=name, align_bytes=ALIGN)
 
-        def bf16_values(width, name, tag=None):
-            return held.tile([P, PACK * width], BF16, name=name, tag=tag or name, align_bytes=256)
+        def rounded(width, name):
+            return held.tile([P, SLOTS * width], BF16, name=name, align_bytes=ALIGN)
 
-        def raw_rows(width, name):
-            return held.tile([P, PACK, width], F32, name=name, align_bytes=256)
+        def slot_rows(width, name):
+            return held.tile([P, SLOTS, width], F32, name=name, align_bytes=ALIGN)
+
+        def bank_tile(shape, name, bank):
+            return psum.tile(shape, F32, name=name, offset=BANK_BYTES * bank)
 
         offsets = held.tile([P, S // 16], U16, name="offsets")
-        planes = [held.tile([P, T], F32, name=f"plane{j}", align_bytes=256) for j in range(PACK)]
-        picked = raw_rows(S, "picked")
-        x_bf = [bf16_values(PIECE, f"x_bf{s}") for s in range(PIECES)]
+        x_all = [held.tile([P, T], F32, name=f"x_all{j}", align_bytes=ALIGN) for j in range(SLOTS)]
+        picked = slot_rows(S, "picked")
+        x_bf = [rounded(PIECE, f"x_bf{s}") for s in range(PIECES)]
         x_codes = {}
         x_scales = scale_bytes(S, "x_scales")
-        w1_raw = [raw_rows(HALF, f"w1_raw{g}") for g in range(HALVES)]
-        w1_bf = {}
+        w1_raw = [slot_rows(HALF, f"w1_raw{g}") for g in range(HALVES)]
         w1_codes = [words(HALF, f"w1_codes{g}") for g in range(HALVES)]
         w1_scales = [scale_bytes(HALF, f"w1_scales{g}") for g in range(HALVES)]
-        w2_first = raw_rows(N, "w2_first")
-        w2_second = [raw_rows(PART, f"w2_second{a}") for a in range(N // PART)]
+        w2_first = slot_rows(N, "w2_first")
+        w2_second = [slot_rows(PART, f"w2_second{part}") for part in range(N // PART)]
         w2_bf = {}
         w2_codes = [words(N, f"w2_codes{g}") for g in range(HALVES)]
         w2_scales = [scale_bytes(N, f"w2_scales{g}") for g in range(HALVES)]
-        h_bf = [[bf16_values(PIECE, f"h_bf{g}{s}") for s in range(PIECES)] for g in range(HALVES)]
+        h_bf = [[rounded(PIECE, f"h_bf{g}{s}") for s in range(PIECES)] for g in range(HALVES)]
         h_codes = {}
         h_scales = [scale_bytes(S, f"h_scales{g}") for g in range(HALVES)]
 
-        x_rows = xT.rearrange("(p j) w -> p j w", j=PACK)
-        w1_rows = w1.rearrange("(p j) i -> p j i", j=PACK)
-        w2_rows = w2.rearrange("(g u a r) m -> g a u r m", g=HALVES, a=PAIR, r=PACK)
-
-        def load_plane(j, lo, hi):
-            nc.sync.dma_start(planes[j][:, lo:hi], x_rows[:, j, lo:hi])
-
-        load_plane(0, 0, T)
+        x_rows = xT.rearrange("(p j) w -> p j w", j=SLOTS)
+        w1_rows = w1.rearrange("(p j) i -> p j i", j=SLOTS)
+        w2_rows = w2.rearrange("(g u a r) m -> g a u r m", g=HALVES, a=TWO, r=TWO * TWO)
+        reach = T - S + PIECE
+        nc.sync.dma_start(x_all[0][:], x_rows[:, 0, :])
         nc.sync.dma_start(offsets[:], offs)
-        load_plane(1, 0, T)
-        load_plane(2, 0, T)
-        load_plane(3, 0, T - S + PIECE)
-        load_plane(3, T - S + PIECE, T)
+        for j in range(1, SLOTS - 1):
+            nc.sync.dma_start(x_all[j][:], x_rows[:, j, :])
+        nc.sync.dma_start(x_all[SLOTS - 1][:, :reach], x_rows[:, SLOTS - 1, :reach])
+        nc.sync.dma_start(x_all[SLOTS - 1][:, reach:], x_rows[:, SLOTS - 1, reach:])
         for g in range(HALVES):
             nc.sync.dma_start(w1_raw[g][:], w1_rows[:, :, HALF * g : HALF * (g + 1)])
 
         def load_w2(raw, g, lo, hi):
-            for a in range(PAIR):
-                slots = raw[:, PAIR * a : PAIR * (a + 1), :].rearrange("p b m -> p (b m)")
-                nc.sync.dma_start(slots, w2_rows[g, a][:, :, lo:hi])
+            for a in range(TWO):
+                pair = raw[:, TWO * a : TWO * (a + 1), :].rearrange("p b m -> p (b m)")
+                nc.sync.dma_start(pair, w2_rows[g, a][:, :, lo:hi])
 
         load_w2(w2_first, 0, 0, N)
         for part in range(N // PART):
@@ -97,200 +99,194 @@ def tile_picked_pick_mlp_relu_srt_e_kernel(tc, xT, w1, w2, offs, out):
         nc.vector.memset(warm_in[:], 0.0)
         nc.scalar.activation(warm_out[:], warm_in[:], RELU)
 
-        def copy(engine, dst, src):
-            if engine == "scalar":
-                nc.scalar.copy(dst, src)
-            else:
-                nc.vector.tensor_copy(dst, src)
-
         def quantise(codes, scales, values):
             nc.vector.quantize_mx(out=codes.bitcast(FP8X4), scales=scales, in_=values)
 
-        def gather(j, lo, hi):
-            nc.vector.tensor_copy(
-                picked[:, j, lo:hi], planes[j][:, : T - S + hi].indirect(offsets[:, lo // 16 : hi // 16])
+        def interleave(dst, src):
+            on_vector(
+                dst.rearrange("p (q c j) -> p q j c", c=RUN, j=SLOTS), src.rearrange("p j (q c) -> p q j c", c=RUN)
             )
 
-        def cast_x(engine, u, s):
-            dst = x_bf[s][:].rearrange("p (q c u e) -> p u q e c", c=RUN, u=PAIR, e=PAIR)[:, u]
-            src = picked[:, PAIR * u : PAIR * (u + 1), PIECE * s : PIECE * (s + 1)]
-            copy(engine, dst, src.rearrange("p e (q c) -> p q e c", c=RUN))
+        def gather(j, lo, hi):
+            on_vector(picked[:, j, lo:hi], x_all[j][:, : T - S + hi].indirect(offsets[:, lo // 16 : hi // 16]))
 
-        def cast_x_whole(s):
-            dst = x_bf[s][:].rearrange("p (q c j) -> p q j c", c=RUN, j=PACK)
-            src = picked[:, :, PIECE * s : PIECE * (s + 1)]
-            nc.vector.tensor_copy(dst, src.rearrange("p j (q c) -> p q j c", c=RUN))
+        def round_x_pair(a, s):
+            dst = x_bf[s][:].rearrange("p (q c a b) -> p a q b c", c=RUN, a=TWO, b=TWO)[:, a]
+            src = picked[:, TWO * a : TWO * (a + 1), PIECE * s : PIECE * (s + 1)]
+            on_scalar(dst, src.rearrange("p b (q c) -> p q b c", c=RUN))
 
-        def quantise_x(lo, hi, behind_w1):
-            if behind_w1:
-                codes = shared.tile([P, hi - lo], U32, name=f"x_codes{lo}", align_bytes=256, offset=4 * (lo - BLOCK))
-            else:
-                codes = words(hi - lo, f"x_codes{lo}")
-            for b in range(lo, hi, BLOCK):
-                x_codes[b] = codes[:, b - lo : b - lo + BLOCK]
-            first = PACK * (lo % PIECE)
-            quantise(codes[:], x_scales[:, lo:hi], x_bf[lo // PIECE][:, first : first + PACK * (hi - lo)])
+        def quantise_x(codes, lo, hi):
+            for first in range(lo, hi, BLOCK):
+                x_codes[first // BLOCK] = codes[:, first - lo : first - lo + BLOCK]
+            start = SLOTS * (lo % PIECE)
+            quantise(codes[:], x_scales[:, lo:hi], x_bf[lo // PIECE][:, start : start + SLOTS * (hi - lo)])
 
-        def cast_w1(engine, g, u, lo, hi, offset=None):
-            name = f"w1_bf{g}{u}{lo}"
-            if offset is None:
-                values = bf16_values(PAIR * (hi - lo), name)
-            else:
-                values = shared.tile([P, PACK * PAIR * (hi - lo)], BF16, name=name, align_bytes=256, offset=offset)
-            w1_bf[g, u, lo] = values
-            src = w1_raw[g][:].rearrange("p j (v a c b) -> p a v b j c", a=PAIR, c=PAIR, b=PAIR)[:, u]
-            dst = values[:].rearrange("p (b v c j) -> p v b j c", b=PAIR, c=PAIR, j=PACK)
-            copy(engine, dst, src[:, lo // PAIR : hi // PAIR])
+        def round_w1_pair(values, g, a):
+            src = w1_raw[g][:].rearrange("p j (u a c b) -> p a u b j c", a=TWO, c=TWO, b=TWO)[:, a]
+            on_vector(values[:].rearrange("p (b u c j) -> p u b j c", b=TWO, c=TWO, j=SLOTS), src)
 
-        def quantise_w1(g, u):
-            columns = slice(PAIR * P * u, PAIR * P * (u + 1))
-            quantise(w1_codes[g][:, columns], w1_scales[g][:, columns], w1_bf[g, u, 0][:])
+        def round_w1_tile(copy, t, lo, hi):
+            values = rounded(hi - lo, f"w1_bf_tile{t}_{lo}")
+            src = w1_raw[0][:].rearrange("p j (u a c b) -> p a b u j c", a=TWO, c=TWO, b=TWO)[:, t // TWO, t % TWO]
+            copy(values[:].rearrange("p (u c j) -> p u j c", c=TWO, j=SLOTS), src[:, lo // TWO : hi // TWO])
+            return values
 
-        def quantise_w1_part(g, u, e, lo, hi):
-            first = P * (PAIR * u + e)
-            columns = slice(first + lo, first + hi)
-            values = w1_bf[g, u, lo][:, PACK * (hi - lo) * e : PACK * (hi - lo) * (e + 1)]
-            quantise(w1_codes[g][:, columns], w1_scales[g][:, columns], values)
+        def quantise_w1(g, lo, hi, values):
+            quantise(w1_codes[g][:, lo:hi], w1_scales[g][:, lo:hi], values)
 
-        def cast_w2(engine, g, lo, hi, tag=None):
+        def round_w2(g, lo, hi):
             src = w2_first[:, :, lo:hi] if g == 0 else w2_second[lo // PART][:, :, lo % PART : lo % PART + hi - lo]
-            w2_bf[g, lo] = bf16_values(hi - lo, f"w2_bf{g}_{lo}", tag)
-            dst = w2_bf[g, lo][:].rearrange("p (q c j) -> p q j c", c=RUN, j=PACK)
-            copy(engine, dst, src.rearrange("p j (q c) -> p q j c", c=RUN))
+            w2_bf[g, lo] = rounded(hi - lo, f"w2_bf{g}_{lo}")
+            interleave(w2_bf[g, lo][:], src)
 
         def quantise_w2(g, lo, hi):
             quantise(w2_codes[g][:, lo:hi], w2_scales[g][:, lo:hi], w2_bf[g, lo][:])
 
-        def layer1_block(g, lo, number):
-            bank = psum.tile([P, PACK, BLOCK], F32, name=f"hidden{g}_{lo}", offset=BANK_BYTES * number)
-            tokens = slice(lo, lo + BLOCK)
-            for t in range(PACK):
-                channels = slice(P * t, P * (t + 1))
+        def hidden_block(g, block, bank):
+            tiles = bank_tile([P, SLOTS, BLOCK], f"hidden{g}_{block}", bank)
+            for t in range(SLOTS):
+                columns = slice(P * t, P * (t + 1))
                 nc.tensor.matmul_mx(
-                    out=bank[:, t, :],
-                    lhsT=w1_codes[g][:, channels].bitcast(FP8X4),
-                    lhsT_scale=w1_scales[g][:, channels],
-                    rhs=x_codes[lo].bitcast(FP8X4),
-                    rhs_scale=x_scales[:, tokens],
+                    out=tiles[:, t, :],
+                    lhsT=w1_codes[g][:, columns].bitcast(FP8X4),
+                    lhsT_scale=w1_scales[g][:, columns],
+                    rhs=x_codes[block].bitcast(FP8X4),
+                    rhs_scale=x_scales[:, BLOCK * block : BLOCK * (block + 1)],
                     start=True,
                     stop=True,
                 )
-            first = PACK * (lo % PIECE)
-            dst = h_bf[g][lo // PIECE][:, first : first + PACK * BLOCK].rearrange("p (n t) -> p n t", t=PACK)
-            nc.scalar.activation(dst, bank[:].rearrange("p t n -> p n t"), RELU)
+            s, place = divmod(block, PIECE // BLOCK)
+            dst = h_bf[g][s][:, SLOTS * BLOCK * place : SLOTS * BLOCK * (place + 1)]
+            nc.scalar.activation(dst.rearrange("p (n t) -> p n t", t=SLOTS), tiles[:].rearrange("p t n -> p n t"), RELU)
 
-        def quantise_h(g, s, tag=None):
-            tokens = slice(PIECE * s, PIECE * (s + 1))
-            h_codes[g, s] = words(PIECE, f"h_codes{g}{s}", tag)
-            quantise(h_codes[g, s][:], h_scales[g][:, tokens], h_bf[g][s][:])
+        def quantise_h(g, s, after=None):
+            h_codes[g, s] = words(PIECE, f"h_codes{g}{s}", after)
+            quantise(h_codes[g, s][:], h_scales[g][:, PIECE * s : PIECE * (s + 1)], h_bf[g][s][:])
 
-        banks = {}
+        sums = {}
 
-        def layer2_pass(g, number, parts, opens, only=None):
-            if opens:
-                banks[parts] = psum.tile(
-                    [P, len(parts), PIECE], F32, name=f"sum{parts[0][0]}{parts[0][1]}", offset=BANK_BYTES * number
-                )
-            for d, (m, s) in enumerate(parts):
-                if only is not None and d != only:
-                    continue
-                rows = slice(P * m, P * (m + 1))
-                nc.tensor.matmul_mx(
-                    out=banks[parts][:, d, :],
-                    lhsT=w2_codes[g][:, rows].bitcast(FP8X4),
-                    lhsT_scale=w2_scales[g][:, rows],
-                    rhs=h_codes[g, s][:].bitcast(FP8X4),
-                    rhs_scale=h_scales[g][:, PIECE * s : PIECE * (s + 1)],
-                    start=(opens and d == 0),
-                    stop=(not opens and d == len(parts) - 1),
-                )
+        def output_pass(g, group, place):
+            m, s = group[place]
+            rows = slice(P * m, P * (m + 1))
+            nc.tensor.matmul_mx(
+                out=sums[group][:, place, :],
+                lhsT=w2_codes[g][:, rows].bitcast(FP8X4),
+                lhsT_scale=w2_scales[g][:, rows],
+                rhs=h_codes[g, s][:].bitcast(FP8X4),
+                rhs_scale=h_scales[g][:, PIECE * s : PIECE * (s + 1)],
+                start=(g == 0 and place == 0),
+                stop=(g == HALVES - 1 and place == len(group) - 1),
+            )
 
-        def store_rows(m, first, second):
-            result = held.tile([P, PIECES, PIECE], F32, name=f"rows{m}", align_bytes=256)
-            copy(first, result[:, : PIECES - 1, :], banks[(m, 0), (m, 1)][:])
-            copy(second, result[:, PIECES - 1 :, :], banks[((m, 2),)][:])
-            nc.sync.dma_start(out[P * m : P * (m + 1), :], result[:].rearrange("p d n -> p (d n)"))
+        def open_group(group, bank):
+            m, s = group[0]
+            sums[group] = bank_tile([P, len(group), PIECE], f"sum{m}{s}", bank)
+            for place in range(len(group)):
+                output_pass(0, group, place)
 
-        def store(engine, parts):
-            (m, s), (last_m, last_s) = parts[0], parts[-1]
-            result = held.tile([P, len(parts), PIECE], F32, name=f"result{m}{s}", align_bytes=256)
-            copy(engine, result[:], banks[parts][:])
-            rows = out[P * m : P * (last_m + 1), PIECE * s : PIECE * (last_s + 1)]
-            if last_m > m:
-                nc.sync.dma_start(rows.rearrange("(d p) n -> p d n", d=len(parts)), result[:])
-            else:
-                nc.sync.dma_start(rows, result[:].rearrange("p d n -> p (d n)"))
+        def close_group(group):
+            for place in range(len(group)):
+                output_pass(1, group, place)
+
+        def staged(parts, name):
+            return held.tile([P, parts, PIECE], F32, name=name, align_bytes=ALIGN)
+
+        def store_tokens(copy, group):
+            m, s = group[0]
+            result = staged(len(group), f"result{m}{s}")
+            copy(result[:], sums[group][:])
+            rows = out[P * m : P * (m + 1), PIECE * s : PIECE * (s + len(group))]
+            nc.sync.dma_start(rows, result[:].rearrange("p d n -> p (d n)"))
+
+        early = [tuple((m, s) for s in range(LAST)) for m in range(N // P)]
+        late_pair = ((0, LAST), (1, LAST))
+        late = {m: ((m, LAST),) for m in (2, 3)}
 
         gather(0, 0, S)
         gather(1, 0, S)
-        for s in range(PIECES - 1):
-            cast_x("scalar", 0, s)
+        for s in range(LAST):
+            round_x_pair(0, s)
         gather(2, 0, S)
         for s in range(PIECES):
-            gather(PACK - 1, PIECE * s, PIECE * (s + 1))
-        cast_x("scalar", 1, 0)
-        cast_x("scalar", 1, 1)
-        quantise_x(0, BLOCK, False)
-        cast_x_whole(2)
-        cast_w1("vector", 0, 0, 0, P, 0)
-        cast_w1("scalar", 0, 1, SHARE, P)
-        cast_w1("vector", 0, 1, 0, SHARE)
-        quantise_w1(0, 0)
-        for e in range(PAIR):
-            quantise_w1_part(0, 1, e, 0, SHARE)
-            quantise_w1_part(0, 1, e, SHARE, P)
-        quantise_x(BLOCK, PIECE, True)
-        quantise_x(PIECE, WIDE, True)
-        quantise_x(WIDE, S, True)
-        wide = [((m, 0), (m, 1)) for m in range(N // P)]
-        top = ((0, 2), (1, 2))
-        last = {m: ((m, 2),) for m in (2, 3)}
-        for b in range(5):
-            layer1_block(0, BLOCK * b, b)
-        cast_w1("vector", 1, 0, 0, P)
-        cast_w1("vector", 1, 1, 0, P)
-        quantise_w1(1, 0)
-        quantise_w1(1, 1)
-        for b in range(4):
-            layer1_block(1, BLOCK * b, (5 + b) % BANKS)
-        layer1_block(0, S - BLOCK, 5)
-        for b in range(4, 6):
-            layer1_block(1, BLOCK * b, b - 3)
+            gather(SLOTS - 1, PIECE * s, PIECE * (s + 1))
+        for s in range(LAST):
+            round_x_pair(1, s)
+        quantise_x(words(BLOCK, "x_codes0"), 0, BLOCK)
+        interleave(x_bf[LAST][:], picked[:, :, PIECE * LAST :])
+
+        first_pair = overlaid.tile([P, TWO * HALF], BF16, name="w1_bf_first_pair", align_bytes=ALIGN, offset=0)
+        round_w1_pair(first_pair, 0, 0)
+        tile2_high = round_w1_tile(on_scalar, 2, SPLIT, P)
+        tile3 = round_w1_tile(on_scalar, 3, 0, P)
+        tile2_low = round_w1_tile(on_vector, 2, 0, SPLIT)
+        for t in range(TWO):
+            quantise_w1(0, P * t, P * (t + 1), first_pair[:, HALF * t : HALF * (t + 1)])
+        quantise_w1(0, 2 * P, 2 * P + SPLIT, tile2_low[:])
+        quantise_w1(0, 2 * P + SPLIT, 3 * P, tile2_high[:])
+        quantise_w1(0, 3 * P, HALF, tile3[:])
+
+        for lo, hi in ((BLOCK, PIECE), (PIECE, 2 * PIECE), (2 * PIECE, S)):
+            codes = overlaid.tile([P, hi - lo], U32, name=f"x_codes{lo}", align_bytes=ALIGN, offset=4 * (lo - BLOCK))
+            quantise_x(codes, lo, hi)
+
+        early_blocks = LAST * PIECE // BLOCK
+        for block in range(BLOCKS - 1):
+            hidden_block(0, block, block)
+        second_pairs = [rounded(TWO * P, f"w1_bf_second_pair{a}") for a in range(TWO)]
+        for a in range(TWO):
+            round_w1_pair(second_pairs[a], 1, a)
+        for a in range(TWO):
+            quantise_w1(1, TWO * P * a, TWO * P * (a + 1), second_pairs[a][:])
+        for block in range(early_blocks):
+            hidden_block(1, block, (BLOCKS - 1 + block) % BANKS)
+        hidden_block(0, BLOCKS - 1, BLOCKS - 1)
+        for block in range(early_blocks, BLOCKS):
+            hidden_block(1, block, (BLOCKS - 1 + block) % BANKS)
+
         quantise_h(0, 0)
-        cast_w2("vector", 0, 0, PART)
-        cast_w2("vector", 0, PART, N)
+        quantise_h(0, 1)
+        round_w2(0, 0, PART)
+        round_w2(0, PART, N)
         quantise_w2(0, 0, PART)
-        cast_w2("vector", 1, 0, PART)
-        quantise_h(0, 1, "w2_first")
-        layer2_pass(0, 3, wide[0], True)
-        layer2_pass(0, 4, wide[1], True)
-        quantise_h(1, 0, "w2_second0")
+        open_group(early[0], 3)
+        open_group(early[1], 4)
+        round_w2(1, 0, PART)
+        quantise_h(1, 0, after="w2_first")
         quantise_w2(1, 0, PART)
-        layer2_pass(1, 3, wide[0], False, 0)
-        layer2_pass(1, 4, wide[1], False, 0)
-        quantise_h(1, 1, "w2_bf0_0")
-        layer2_pass(1, 3, wide[0], False, 1)
-        layer2_pass(1, 4, wide[1], False, 1)
-        store("scalar", wide[0])
-        store("scalar", wide[1])
+        for m in range(TWO):
+            output_pass(1, early[m], 0)
+        quantise_h(1, 1, after="w2_second0")
+        for m in range(TWO):
+            output_pass(1, early[m], 1)
+        for m in range(TWO):
+            store_tokens(on_scalar, early[m])
+
         quantise_w2(0, PART, N)
-        layer2_pass(0, 7, wide[2], True)
-        layer2_pass(0, 6, wide[3], True)
-        cast_w2("vector", 1, 2 * P, 3 * P)
-        quantise_h(0, 2, "w2_bf1_0")
+        open_group(early[2], 7)
+        open_group(early[3], 6)
+        round_w2(1, 2 * P, 3 * P)
+        quantise_h(0, LAST, after="w2_bf1_0")
         quantise_w2(1, 2 * P, 3 * P)
-        layer2_pass(1, 7, wide[2], False)
-        store("scalar", wide[2])
-        layer2_pass(0, 0, last[2], True)
-        layer2_pass(0, 5, top, True)
-        layer2_pass(0, 1, last[3], True)
-        cast_w2("vector", 1, 3 * P, N)
-        quantise_h(1, 2)
-        layer2_pass(1, 0, last[2], False)
-        layer2_pass(1, 5, top, False)
+        close_group(early[2])
+        store_tokens(on_scalar, early[2])
+
+        open_group(late[2], 0)
+        open_group(late_pair, 5)
+        open_group(late[3], 1)
+        round_w2(1, 3 * P, N)
+        quantise_h(1, LAST)
+        close_group(late[2])
+        close_group(late_pair)
         quantise_w2(1, 3 * P, N)
-        layer2_pass(1, 6, wide[3], False)
-        layer2_pass(1, 1, last[3], False)
-        store("scalar", last[2])
-        store("vector", top)
-        store_rows(3, "scalar", "vector")
+        close_group(early[3])
+        close_group(late[3])
+        store_tokens(on_scalar, late[2])
+
+        pair_result = staged(TWO, "pair_result")
+        on_vector(pair_result[:], sums[late_pair][:])
+        nc.sync.dma_start(out[: TWO * P, PIECE * LAST :].rearrange("(d p) n -> p d n", d=TWO), pair_result[:])
+
+        whole_rows = staged(PIECES, "whole_rows")
+        on_scalar(whole_rows[:, :LAST, :], sums[early[3]][:])
+        on_vector(whole_rows[:, LAST:, :], sums[late[3]][:])
+        nc.sync.dma_start(out[3 * P :, :], whole_rows[:].rearrange("p d n -> p (d n)"))

@@ -51,8 +51,11 @@ def tile_picked_pick_mlp_relu_srt_e_kernel(tc, xT, w1, w2, offs, out):
         def slot_rows(width, name):
             return held.tile([P, SLOTS, width], F32, name=name, align_bytes=ALIGN)
 
-        def bank_tile(shape, name, bank):
-            return psum.tile(shape, F32, name=name, offset=BANK_BYTES * bank)
+        bank_users = []
+
+        def next_bank(shape, name):
+            bank_users.append(psum.tile(shape, F32, name=name, offset=BANK_BYTES * (len(bank_users) % BANKS)))
+            return bank_users[-1]
 
         offsets = held.tile([P, S // 16], U16, name="offsets")
         x_all = [held.tile([P, T], F32, name=f"x_all{j}", align_bytes=ALIGN) for j in range(SLOTS)]
@@ -142,8 +145,8 @@ def tile_picked_pick_mlp_relu_srt_e_kernel(tc, xT, w1, w2, offs, out):
         def quantise_w2(g, lo, hi):
             quantise(w2_codes[g][:, lo:hi], w2_scales[g][:, lo:hi], w2_bf[g, lo][:])
 
-        def hidden_block(g, block, bank):
-            tiles = bank_tile([P, SLOTS, BLOCK], f"hidden{g}_{block}", bank)
+        def hidden_block(g, block):
+            tiles = next_bank([P, SLOTS, BLOCK], f"hidden{g}_{block}")
             for t in range(SLOTS):
                 columns = slice(P * t, P * (t + 1))
                 nc.tensor.matmul_mx(
@@ -159,9 +162,11 @@ def tile_picked_pick_mlp_relu_srt_e_kernel(tc, xT, w1, w2, offs, out):
             dst = h_bf[g][s][:, SLOTS * BLOCK * place : SLOTS * BLOCK * (place + 1)]
             nc.scalar.activation(dst.rearrange("p (n t) -> p n t", t=SLOTS), tiles[:].rearrange("p t n -> p n t"), RELU)
 
-        def quantise_h(g, s, after=None):
+        def quantise_h(g, s, after=None, width=PIECE):
             h_codes[g, s] = words(PIECE, f"h_codes{g}{s}", after)
-            quantise(h_codes[g, s][:], h_scales[g][:, PIECE * s : PIECE * (s + 1)], h_bf[g][s][:])
+            for lo in range(0, PIECE, width):
+                scales = h_scales[g][:, PIECE * s + lo : PIECE * s + lo + width]
+                quantise(h_codes[g, s][:, lo : lo + width], scales, h_bf[g][s][:, SLOTS * lo : SLOTS * (lo + width)])
 
         sums = {}
 
@@ -178,9 +183,9 @@ def tile_picked_pick_mlp_relu_srt_e_kernel(tc, xT, w1, w2, offs, out):
                 stop=(g == HALVES - 1 and place == len(group) - 1),
             )
 
-        def open_group(group, bank):
+        def open_group(group):
             m, s = group[0]
-            sums[group] = bank_tile([P, len(group), PIECE], f"sum{m}{s}", bank)
+            sums[group] = next_bank([P, len(group), PIECE], f"sum{m}{s}")
             for place in range(len(group)):
                 output_pass(0, group, place)
 
@@ -229,50 +234,46 @@ def tile_picked_pick_mlp_relu_srt_e_kernel(tc, xT, w1, w2, offs, out):
             codes = overlaid.tile([P, hi - lo], U32, name=f"x_codes{lo}", align_bytes=ALIGN, offset=4 * (lo - BLOCK))
             quantise_x(codes, lo, hi)
 
-        early_blocks = LAST * PIECE // BLOCK
-        for block in range(BLOCKS - 1):
-            hidden_block(0, block, block)
+        for block in range(BLOCKS):
+            hidden_block(0, block)
         second_pairs = [rounded(TWO * P, f"w1_bf_second_pair{a}") for a in range(TWO)]
         for a in range(TWO):
             round_w1_pair(second_pairs[a], 1, a)
         for a in range(TWO):
             quantise_w1(1, TWO * P * a, TWO * P * (a + 1), second_pairs[a][:])
-        for block in range(early_blocks):
-            hidden_block(1, block, (BLOCKS - 1 + block) % BANKS)
-        hidden_block(0, BLOCKS - 1, BLOCKS - 1)
-        for block in range(early_blocks, BLOCKS):
-            hidden_block(1, block, (BLOCKS - 1 + block) % BANKS)
+        for block in range(BLOCKS):
+            hidden_block(1, block)
 
         quantise_h(0, 0)
         quantise_h(0, 1)
         round_w2(0, 0, PART)
         round_w2(0, PART, N)
         quantise_w2(0, 0, PART)
-        open_group(early[0], 3)
-        open_group(early[1], 4)
+        open_group(early[0])
+        open_group(early[1])
         round_w2(1, 0, PART)
         quantise_h(1, 0, after="w2_first")
         quantise_w2(1, 0, PART)
         for m in range(TWO):
             output_pass(1, early[m], 0)
-        quantise_h(1, 1, after="w2_second0")
+        quantise_h(1, 1, after="w2_bf0_0", width=BLOCK)
         for m in range(TWO):
             output_pass(1, early[m], 1)
         for m in range(TWO):
             store_tokens(on_scalar, early[m])
 
         quantise_w2(0, PART, N)
-        open_group(early[2], 7)
-        open_group(early[3], 6)
+        open_group(early[2])
+        open_group(early[3])
         round_w2(1, 2 * P, 3 * P)
         quantise_h(0, LAST, after="w2_bf1_0")
         quantise_w2(1, 2 * P, 3 * P)
         close_group(early[2])
         store_tokens(on_scalar, early[2])
 
-        open_group(late[2], 0)
-        open_group(late_pair, 5)
-        open_group(late[3], 1)
+        open_group(late[2])
+        open_group(late_pair)
+        open_group(late[3])
         round_w2(1, 3 * P, N)
         quantise_h(1, LAST)
         close_group(late[2])

@@ -16,7 +16,7 @@ LAST = PIECES - 1
 BLOCK = 128
 BLOCKS = S // BLOCK
 PART = 256
-SPLIT = 64
+SPLIT = 32
 RUN = 2
 BANK_BYTES = 2048
 BANKS = 8
@@ -124,15 +124,10 @@ def tile_picked_pick_mlp_relu_srt_e_kernel(tc, xT, w1, w2, offs, out):
             start = SLOTS * (lo % PIECE)
             quantise(codes[:], x_scales[:, lo:hi], x_bf[lo // PIECE][:, start : start + SLOTS * (hi - lo)])
 
-        def round_w1_pair(values, g, a):
+        def round_w1_pair(values, g, a, copy=on_vector, lo=0, hi=P):
             src = w1_raw[g][:].rearrange("p j (u a c b) -> p a u b j c", a=TWO, c=TWO, b=TWO)[:, a]
-            on_vector(values[:].rearrange("p (b u c j) -> p u b j c", b=TWO, c=TWO, j=SLOTS), src)
-
-        def round_w1_tile(copy, t, lo, hi):
-            values = rounded(hi - lo, f"w1_bf_tile{t}_{lo}")
-            src = w1_raw[0][:].rearrange("p j (u a c b) -> p a b u j c", a=TWO, c=TWO, b=TWO)[:, t // TWO, t % TWO]
-            copy(values[:].rearrange("p (u c j) -> p u j c", c=TWO, j=SLOTS), src[:, lo // TWO : hi // TWO])
-            return values
+            dst = values[:].rearrange("p (b u c j) -> p u b j c", b=TWO, c=TWO, j=SLOTS)
+            copy(dst[:, lo // TWO : hi // TWO], src[:, lo // TWO : hi // TWO])
 
         def quantise_w1(g, lo, hi, values):
             quantise(w1_codes[g][:, lo:hi], w1_scales[g][:, lo:hi], values)
@@ -221,14 +216,13 @@ def tile_picked_pick_mlp_relu_srt_e_kernel(tc, xT, w1, w2, offs, out):
 
         first_pair = overlaid.tile([P, TWO * HALF], BF16, name="w1_bf_first_pair", align_bytes=ALIGN, offset=0)
         round_w1_pair(first_pair, 0, 0)
-        tile2_high = round_w1_tile(on_scalar, 2, SPLIT, P)
-        tile3 = round_w1_tile(on_scalar, 3, 0, P)
-        tile2_low = round_w1_tile(on_vector, 2, 0, SPLIT)
+        other_pair = rounded(TWO * P, "w1_bf_other_pair")
+        round_w1_pair(other_pair, 0, 1, on_scalar, SPLIT, P)
+        round_w1_pair(other_pair, 0, 1, on_vector, 0, SPLIT)
         for t in range(TWO):
             quantise_w1(0, P * t, P * (t + 1), first_pair[:, HALF * t : HALF * (t + 1)])
-        quantise_w1(0, 2 * P, 2 * P + SPLIT, tile2_low[:])
-        quantise_w1(0, 2 * P + SPLIT, 3 * P, tile2_high[:])
-        quantise_w1(0, 3 * P, HALF, tile3[:])
+        for t in range(TWO):
+            quantise_w1(0, P * (TWO + t), P * (TWO + t + 1), other_pair[:, HALF * t : HALF * (t + 1)])
 
         for lo, hi in ((BLOCK, PIECE), (PIECE, 2 * PIECE), (2 * PIECE, S)):
             codes = overlaid.tile([P, hi - lo], U32, name=f"x_codes{lo}", align_bytes=ALIGN, offset=4 * (lo - BLOCK))

@@ -29,6 +29,7 @@ U16 = mybir.dt.uint16
 U8 = mybir.dt.uint8
 FP8X4 = mybir.dt.float8_e4m3fn_x4
 RELU = mybir.ActivationFunctionType.Relu
+COPY = mybir.ActivationFunctionType.Copy
 
 
 def tile_picked_pick_mlp_relu_srt_e_kernel(tc, xT, w1, w2, offs, out):
@@ -45,8 +46,8 @@ def tile_picked_pick_mlp_relu_srt_e_kernel(tc, xT, w1, w2, offs, out):
         def scale_bytes(width, name):
             return held.tile([P, width], U8, name=name, align_bytes=ALIGN)
 
-        def rounded(width, name):
-            return held.tile([P, SLOTS * width], BF16, name=name, align_bytes=ALIGN)
+        def rounded(width, name, after=None):
+            return held.tile([P, SLOTS * width], BF16, name=name, tag=after or name, align_bytes=ALIGN)
 
         def slot_rows(width, name):
             return held.tile([P, SLOTS, width], F32, name=name, align_bytes=ALIGN)
@@ -60,7 +61,8 @@ def tile_picked_pick_mlp_relu_srt_e_kernel(tc, xT, w1, w2, offs, out):
         offsets = held.tile([P, S // 16], U16, name="offsets")
         x_all = [held.tile([P, T], F32, name=f"x_all{j}", align_bytes=ALIGN) for j in range(SLOTS)]
         picked = slot_rows(S, "picked")
-        x_bf = [rounded(PIECE, f"x_bf{s}") for s in range(PIECES)]
+        early_runs = ((0, BLOCK), (BLOCK, PIECE), (PIECE, 2 * PIECE))
+        x_bf = {lo: rounded(hi - lo, f"x_bf{lo}") for lo, hi in early_runs}
         x_codes = {}
         x_scales = scale_bytes(S, "x_scales")
         w1_raw = [slot_rows(HALF, f"w1_raw{g}") for g in range(HALVES)]
@@ -110,19 +112,21 @@ def tile_picked_pick_mlp_relu_srt_e_kernel(tc, xT, w1, w2, offs, out):
                 dst.rearrange("p (q c j) -> p q j c", c=RUN, j=SLOTS), src.rearrange("p j (q c) -> p q j c", c=RUN)
             )
 
-        def gather(j, lo, hi):
-            on_vector(picked[:, j, lo:hi], x_all[j][:, : T - S + hi].indirect(offsets[:, lo // 16 : hi // 16]))
+        def gather_on_scalar(dst, src):
+            nc.scalar.activation(dst, src, COPY)
 
-        def round_x_pair(a, s):
-            dst = x_bf[s][:].rearrange("p (q c a b) -> p a q b c", c=RUN, a=TWO, b=TWO)[:, a]
-            src = picked[:, TWO * a : TWO * (a + 1), PIECE * s : PIECE * (s + 1)]
+        def gather(j, lo, hi, copy=on_vector):
+            copy(picked[:, j, lo:hi], x_all[j][:, : T - S + hi].indirect(offsets[:, lo // 16 : hi // 16]))
+
+        def round_x_pair(a, lo, hi):
+            dst = x_bf[lo][:].rearrange("p (q c a b) -> p a q b c", c=RUN, a=TWO, b=TWO)[:, a]
+            src = picked[:, TWO * a : TWO * (a + 1), lo:hi]
             on_scalar(dst, src.rearrange("p b (q c) -> p q b c", c=RUN))
 
         def quantise_x(codes, lo, hi):
             for first in range(lo, hi, BLOCK):
                 x_codes[first // BLOCK] = codes[:, first - lo : first - lo + BLOCK]
-            start = SLOTS * (lo % PIECE)
-            quantise(codes[:], x_scales[:, lo:hi], x_bf[lo // PIECE][:, start : start + SLOTS * (hi - lo)])
+            quantise(codes[:], x_scales[:, lo:hi], x_bf[lo][:])
 
         def round_w1_pair(values, g, a, copy=on_vector, lo=0, hi=P):
             src = w1_raw[g][:].rearrange("p j (u a c b) -> p a u b j c", a=TWO, c=TWO, b=TWO)[:, a]
@@ -204,15 +208,17 @@ def tile_picked_pick_mlp_relu_srt_e_kernel(tc, xT, w1, w2, offs, out):
 
         gather(0, 0, S)
         gather(1, 0, S)
-        for s in range(LAST):
-            round_x_pair(0, s)
-        gather(2, 0, S)
+        for lo, hi in early_runs:
+            round_x_pair(0, lo, hi)
+        gather(2, 0, PIECE * LAST)
+        gather(2, PIECE * LAST, S, gather_on_scalar)
         for s in range(PIECES):
             gather(SLOTS - 1, PIECE * s, PIECE * (s + 1))
-        for s in range(LAST):
-            round_x_pair(1, s)
+        for lo, hi in early_runs:
+            round_x_pair(1, lo, hi)
         quantise_x(words(BLOCK, "x_codes0"), 0, BLOCK)
-        interleave(x_bf[LAST][:], picked[:, :, PIECE * LAST :])
+        x_bf[PIECE * LAST] = rounded(PIECE, "x_bf_last", after="x_bf0")
+        interleave(x_bf[PIECE * LAST][:], picked[:, :, PIECE * LAST :])
 
         first_pair = overlaid.tile([P, TWO * HALF], BF16, name="w1_bf_first_pair", align_bytes=ALIGN, offset=0)
         round_w1_pair(first_pair, 0, 0)

@@ -18,6 +18,7 @@ BLOCKS = S // BLOCK
 PART = 256
 SPLIT = 32
 RUN = 2
+WARM_PASSES = 9
 BANK_BYTES = 2048
 BANKS = 8
 ALIGN = 256
@@ -219,6 +220,18 @@ def tile_picked_pick_mlp_relu_srt_e_kernel(tc, xT, w1, w2, offs, out):
         quantise_x(words(BLOCK, "x_codes0"), 0, BLOCK)
         x_bf[PIECE * LAST] = rounded(PIECE, "x_bf_last", after="x_bf0")
         interleave(x_bf[PIECE * LAST][:], picked[:, :, PIECE * LAST :])
+
+        unread = next_bank([P, SLOTS, BLOCK], "unread")
+        for n in range(WARM_PASSES):
+            nc.tensor.matmul_mx(
+                out=unread[:, n % SLOTS, :],
+                lhsT=x_codes[0].bitcast(FP8X4),
+                lhsT_scale=x_scales[:, :BLOCK],
+                rhs=x_codes[0].bitcast(FP8X4),
+                rhs_scale=x_scales[:, :BLOCK],
+                start=True,
+                stop=True,
+            )
 
         first_pair = overlaid.tile([P, TWO * HALF], BF16, name="w1_bf_first_pair", align_bytes=ALIGN, offset=0)
         round_w1_pair(first_pair, 0, 0)

from contextlib import ExitStack

import concourse.mybir as mybir

K, T, S, H, N = 512, 2048, 768, 1024, 512
FLOPS = 2 * S * K * H + 2 * S * H * N

P = 128
SLOTS = 4
TWO = 2
HALF = P * SLOTS
HALVES = H // HALF
PIECE = 256
PIECES = S // PIECE
LAST = PIECES - 1
BLOCK = 128
BLOCKS = S // BLOCK
PART = 256
SPLIT = 32
RUN = 2
WARM_PASSES = 9
BANK_BYTES = 2048
BANKS = 8
ALIGN = 256

F32 = mybir.dt.float32
BF16 = mybir.dt.bfloat16
U32 = mybir.dt.uint32
U16 = mybir.dt.uint16
U8 = mybir.dt.uint8
FP8X4 = mybir.dt.float8_e4m3fn_x4
RELU = mybir.ActivationFunctionType.Relu
COPY = mybir.ActivationFunctionType.Copy


def tile_picked_pick_mlp_relu_srt_e_kernel(tc, xT, w1, w2, offs, out):
    nc = tc.nc
    on_vector, on_scalar = nc.vector.tensor_copy, nc.scalar.copy
    with ExitStack() as ctx:
        held = ctx.enter_context(tc.tile_pool(name="held", bufs=1))
        overlaid = ctx.enter_context(tc.tile_pool(name="overlaid", bufs=1))
        psum = ctx.enter_context(tc.psum_pool(name="psum", bufs=1))

        def words(width, name, after=None):
            return held.tile([P, width], U32, name=name, tag=after or name, align_bytes=ALIGN)

        def scale_bytes(width, name):
            return held.tile([P, width], U8, name=name, align_bytes=ALIGN)

        def rounded(width, name, after=None):
            return held.tile([P, SLOTS * width], BF16, name=name, tag=after or name, align_bytes=ALIGN)

        def slot_rows(width, name):
            return held.tile([P, SLOTS, width], F32, name=name, align_bytes=ALIGN)

        bank_users = []

        def next_bank(shape, name):
            bank_users.append(psum.tile(shape, F32, name=name, offset=BANK_BYTES * (len(bank_users) % BANKS)))
            return bank_users[-1]

        offsets = held.tile([P, S // 16], U16, name="offsets")
        x_all = [held.tile([P, T], F32, name=f"x_all{j}", align_bytes=ALIGN) for j in range(SLOTS)]
        picked = slot_rows(S, "picked")
        early_runs = ((0, BLOCK), (BLOCK, PIECE), (PIECE, 2 * PIECE))
        x_bf = {lo: rounded(hi - lo, f"x_bf{lo}") for lo, hi in early_runs}
        x_codes = {}
        x_scales = scale_bytes(S, "x_scales")
        w1_raw = [slot_rows(HALF, f"w1_raw{g}") for g in range(HALVES)]
        w1_codes = [words(HALF, f"w1_codes{g}") for g in range(HALVES)]
        w1_scales = [scale_bytes(HALF, f"w1_scales{g}") for g in range(HALVES)]
        w2_first = slot_rows(N, "w2_first")
        w2_second = [slot_rows(PART, f"w2_second{part}") for part in range(N // PART)]
        w2_bf = {}
        w2_codes = [words(N, f"w2_codes{g}") for g in range(HALVES)]
        w2_scales = [scale_bytes(N, f"w2_scales{g}") for g in range(HALVES)]
        h_bf = [[rounded(PIECE, f"h_bf{g}{s}") for s in range(PIECES)] for g in range(HALVES)]
        h_codes = {}
        h_scales = [scale_bytes(S, f"h_scales{g}") for g in range(HALVES)]

        x_rows = xT.rearrange("(p j) w -> p j w", j=SLOTS)
        w1_rows = w1.rearrange("(p j) i -> p j i", j=SLOTS)
        w2_rows = w2.rearrange("(g u a r) m -> g a u r m", g=HALVES, a=TWO, r=TWO * TWO)
        reach = T - S + PIECE
        nc.sync.dma_start(x_all[0][:], x_rows[:, 0, :])
        nc.sync.dma_start(offsets[:], offs)
        for j in range(1, SLOTS - 1):
            nc.sync.dma_start(x_all[j][:], x_rows[:, j, :])
        nc.sync.dma_start(x_all[SLOTS - 1][:, :reach], x_rows[:, SLOTS - 1, :reach])
        nc.sync.dma_start(x_all[SLOTS - 1][:, reach:], x_rows[:, SLOTS - 1, reach:])
        for g in range(HALVES):
            nc.sync.dma_start(w1_raw[g][:], w1_rows[:, :, HALF * g : HALF * (g + 1)])

        def load_w2(raw, g, lo, hi):
            for a in range(TWO):
                pair = raw[:, TWO * a : TWO * (a + 1), :].rearrange("p b m -> p (b m)")
                nc.sync.dma_start(pair, w2_rows[g, a][:, :, lo:hi])

        load_w2(w2_first, 0, 0, N)
        for part in range(N // PART):
            load_w2(w2_second[part], 1, PART * part, PART * (part + 1))

        warm_in = held.tile([P, 1], F32, name="warm_in")
        warm_out = held.tile([P, 1], F32, name="warm_out")
        nc.vector.memset(warm_in[:], 0.0)
        nc.scalar.activation(warm_out[:], warm_in[:], RELU)

        def quantise(codes, scales, values):
            nc.vector.quantize_mx(out=codes.bitcast(FP8X4), scales=scales, in_=values)

        def interleave(dst, src):
            on_vector(
                dst.rearrange("p (q c j) -> p q j c", c=RUN, j=SLOTS), src.rearrange("p j (q c) -> p q j c", c=RUN)
            )

        def gather_on_scalar(dst, src):
            nc.scalar.activation(dst, src, COPY)

        def gather(j, lo, hi, copy=on_vector):
            copy(picked[:, j, lo:hi], x_all[j][:, : T - S + hi].indirect(offsets[:, lo // 16 : hi // 16]))

        def round_x_pair(a, lo, hi):
            dst = x_bf[lo][:].rearrange("p (q c a b) -> p a q b c", c=RUN, a=TWO, b=TWO)[:, a]
            src = picked[:, TWO * a : TWO * (a + 1), lo:hi]
            on_scalar(dst, src.rearrange("p b (q c) -> p q b c", c=RUN))

        def quantise_x(codes, lo, hi):
            for first in range(lo, hi, BLOCK):
                x_codes[first // BLOCK] = codes[:, first - lo : first - lo + BLOCK]
            quantise(codes[:], x_scales[:, lo:hi], x_bf[lo][:])

        def round_w1_pair(values, g, a, copy=on_vector, lo=0, hi=P):
            src = w1_raw[g][:].rearrange("p j (u a c b) -> p a u b j c", a=TWO, c=TWO, b=TWO)[:, a]
            dst = values[:].rearrange("p (b u c j) -> p u b j c", b=TWO, c=TWO, j=SLOTS)
            copy(dst[:, lo // TWO : hi // TWO], src[:, lo // TWO : hi // TWO])

        def quantise_w1(g, lo, hi, values):
            quantise(w1_codes[g][:, lo:hi], w1_scales[g][:, lo:hi], values)

        def round_w2(g, lo, hi):
            src = w2_first[:, :, lo:hi] if g == 0 else w2_second[lo // PART][:, :, lo % PART : lo % PART + hi - lo]
            w2_bf[g, lo] = rounded(hi - lo, f"w2_bf{g}_{lo}")
            interleave(w2_bf[g, lo][:], src)

        def quantise_w2(g, lo, hi):
            quantise(w2_codes[g][:, lo:hi], w2_scales[g][:, lo:hi], w2_bf[g, lo][:])

        def hidden_block(g, block):
            tiles = next_bank([P, SLOTS, BLOCK], f"hidden{g}_{block}")
            for t in range(SLOTS):
                columns = slice(P * t, P * (t + 1))
                nc.tensor.matmul_mx(
                    out=tiles[:, t, :],
                    lhsT=w1_codes[g][:, columns].bitcast(FP8X4),
                    lhsT_scale=w1_scales[g][:, columns],
                    rhs=x_codes[block].bitcast(FP8X4),
                    rhs_scale=x_scales[:, BLOCK * block : BLOCK * (block + 1)],
                    start=True,
                    stop=True,
                )
            s, place = divmod(block, PIECE // BLOCK)
            dst = h_bf[g][s][:, SLOTS * BLOCK * place : SLOTS * BLOCK * (place + 1)]
            nc.scalar.activation(dst.rearrange("p (n t) -> p n t", t=SLOTS), tiles[:].rearrange("p t n -> p n t"), RELU)

        def quantise_h(g, s, after=None, width=PIECE):
            h_codes[g, s] = words(PIECE, f"h_codes{g}{s}", after)
            for lo in range(0, PIECE, width):
                scales = h_scales[g][:, PIECE * s + lo : PIECE * s + lo + width]
                quantise(h_codes[g, s][:, lo : lo + width], scales, h_bf[g][s][:, SLOTS * lo : SLOTS * (lo + width)])

        sums = {}

        def output_pass(g, group, place):
            m, s = group[place]
            rows = slice(P * m, P * (m + 1))
            nc.tensor.matmul_mx(
                out=sums[group][:, place, :],
                lhsT=w2_codes[g][:, rows].bitcast(FP8X4),
                lhsT_scale=w2_scales[g][:, rows],
                rhs=h_codes[g, s][:].bitcast(FP8X4),
                rhs_scale=h_scales[g][:, PIECE * s : PIECE * (s + 1)],
                start=(g == 0 and place == 0),
                stop=(g == HALVES - 1 and place == len(group) - 1),
            )

        def open_group(group):
            m, s = group[0]
            sums[group] = next_bank([P, len(group), PIECE], f"sum{m}{s}")
            for place in range(len(group)):
                output_pass(0, group, place)

        def close_group(group):
            for place in range(len(group)):
                output_pass(1, group, place)

        def staged(parts, name):
            return held.tile([P, parts, PIECE], F32, name=name, align_bytes=ALIGN)

        def store_tokens(copy, group):
            m, s = group[0]
            result = staged(len(group), f"result{m}{s}")
            copy(result[:], sums[group][:])
            rows = out[P * m : P * (m + 1), PIECE * s : PIECE * (s + len(group))]
            nc.sync.dma_start(rows, result[:].rearrange("p d n -> p (d n)"))

        early = [tuple((m, s) for s in range(LAST)) for m in range(N // P)]
        late_pair = ((0, LAST), (1, LAST))
        late = {m: ((m, LAST),) for m in (2, 3)}

        gather(0, 0, S)
        gather(1, 0, S)
        for lo, hi in early_runs:
            round_x_pair(0, lo, hi)
        gather(2, 0, PIECE * LAST)
        gather(2, PIECE * LAST, S, gather_on_scalar)
        for s in range(PIECES):
            gather(SLOTS - 1, PIECE * s, PIECE * (s + 1))
        for lo, hi in early_runs:
            round_x_pair(1, lo, hi)
        quantise_x(words(BLOCK, "x_codes0"), 0, BLOCK)
        x_bf[PIECE * LAST] = rounded(PIECE, "x_bf_last", after="x_bf0")
        interleave(x_bf[PIECE * LAST][:], picked[:, :, PIECE * LAST :])

        unread = next_bank([P, SLOTS, BLOCK], "unread")
        for n in range(WARM_PASSES):
            nc.tensor.matmul_mx(
                out=unread[:, n % SLOTS, :],
                lhsT=x_codes[0].bitcast(FP8X4),
                lhsT_scale=x_scales[:, :BLOCK],
                rhs=x_codes[0].bitcast(FP8X4),
                rhs_scale=x_scales[:, :BLOCK],
                start=True,
                stop=True,
            )

        first_pair = overlaid.tile([P, TWO * HALF], BF16, name="w1_bf_first_pair", align_bytes=ALIGN, offset=0)
        round_w1_pair(first_pair, 0, 0)
        other_pair = rounded(TWO * P, "w1_bf_other_pair")
        round_w1_pair(other_pair, 0, 1, on_scalar, SPLIT, P)
        round_w1_pair(other_pair, 0, 1, on_vector, 0, SPLIT)
        for t in range(TWO):
            quantise_w1(0, P * t, P * (t + 1), first_pair[:, HALF * t : HALF * (t + 1)])
        for t in range(TWO):
            quantise_w1(0, P * (TWO + t), P * (TWO + t + 1), other_pair[:, HALF * t : HALF * (t + 1)])

        for lo, hi in ((BLOCK, PIECE), (PIECE, 2 * PIECE), (2 * PIECE, S)):
            codes = overlaid.tile([P, hi - lo], U32, name=f"x_codes{lo}", align_bytes=ALIGN, offset=4 * (lo - BLOCK))
            quantise_x(codes, lo, hi)

        for block in range(BLOCKS):
            hidden_block(0, block)
        second_pairs = [rounded(TWO * P, f"w1_bf_second_pair{a}") for a in range(TWO)]
        for a in range(TWO):
            round_w1_pair(second_pairs[a], 1, a)
        for a in range(TWO):
            quantise_w1(1, TWO * P * a, TWO * P * (a + 1), second_pairs[a][:])
        for block in range(BLOCKS):
            hidden_block(1, block)

        quantise_h(0, 0)
        quantise_h(0, 1)
        round_w2(0, 0, PART)
        round_w2(0, PART, N)
        quantise_w2(0, 0, PART)
        open_group(early[0])
        open_group(early[1])
        round_w2(1, 0, PART)
        quantise_h(1, 0, after="w2_first")
        quantise_w2(1, 0, PART)
        for m in range(TWO):
            output_pass(1, early[m], 0)
        quantise_h(1, 1, after="w2_bf0_0", width=BLOCK)
        for m in range(TWO):
            output_pass(1, early[m], 1)
        for m in range(TWO):
            store_tokens(on_scalar, early[m])

        quantise_w2(0, PART, N)
        open_group(early[2])
        open_group(early[3])
        round_w2(1, 2 * P, 3 * P)
        quantise_h(0, LAST, after="w2_bf1_0")
        quantise_w2(1, 2 * P, 3 * P)
        close_group(early[2])
        store_tokens(on_scalar, early[2])

        open_group(late[2])
        open_group(late_pair)
        open_group(late[3])
        round_w2(1, 3 * P, N)
        quantise_h(1, LAST)
        close_group(late[2])
        close_group(late_pair)
        quantise_w2(1, 3 * P, N)
        close_group(early[3])
        close_group(late[3])
        store_tokens(on_scalar, late[2])

        pair_result = staged(TWO, "pair_result")
        on_vector(pair_result[:], sums[late_pair][:])
        nc.sync.dma_start(out[: TWO * P, PIECE * LAST :].rearrange("(d p) n -> p d n", d=TWO), pair_result[:])

        whole_rows = staged(PIECES, "whole_rows")
        on_scalar(whole_rows[:, :LAST, :], sums[early[3]][:])
        on_vector(whole_rows[:, LAST:, :], sums[late[3]][:])
        nc.sync.dma_start(out[3 * P :, :], whole_rows[:].rearrange("p d n -> p (d n)"))
